import numpy as np
import ml_dtypes


def mxq(x, axis, fmt="e4m3"):
    dtype, down = {"e4m3": (ml_dtypes.float8_e4m3fn, 7), "e5m2": (ml_dtypes.float8_e5m2, 14)}[fmt]
    v = np.moveaxis(np.asarray(x, np.float32).astype(ml_dtypes.bfloat16).astype(np.float64), axis, -1)
    blocks = v.reshape(v.shape[:-1] + (-1, 32))
    amax = np.abs(blocks).max(-1, keepdims=True)
    byte = np.maximum(np.where(amax > 0, np.frexp(amax)[1] - 1 + 127, 0) - down, 1)
    scale = np.exp2(byte - 127.0)
    codes = (blocks / scale).astype(np.float32).astype(dtype).astype(np.float64)
    return np.moveaxis((codes * scale).reshape(v.shape), -1, axis)


WIDE = False


def mx_kscale(k):
    if not WIDE:
        return np.ones(k)
    levels = np.array([10, -10, 5, -5, 0])
    if k % 512:
        return np.exp2(np.random.permutation(np.resize(levels, k // 32))).repeat(32)
    a = np.empty((k // 512, 16))
    for p in range(k // 512):
        a[p, :8] = np.random.permutation(np.resize(levels, 8))
        for g in range(8):
            far = levels[np.abs(levels - a[p, g]) >= 10]
            a[p, g + 8] = far[np.random.randint(len(far))]
    return np.exp2(a.ravel()).repeat(32)


def f64(x):
    return np.asarray(x).astype(np.float64)


def striped(idx):
    return np.tile(idx.reshape(-1, 16).T, (8, 1)).astype(np.uint16)


def unstriped(offs):
    return offs[:16].T.reshape(-1).astype(np.int64)


def relu(v):
    return np.maximum(v, 0.0)


K, T, S, N, U = 512, 2048, 1024, 128, 2048


def setup_inputs():
    n = np.random.standard_normal
    s = mx_kscale(K)[:, None]
    return {
        "xT": (n((K, T)) * s).astype(np.float32),
        "w1": (n((K, N)) / np.sqrt(K) / s).astype(np.float32),
        "res": n((N, U)).astype(np.float32),
        "offs": striped(np.random.permutation(T)[:S]),
        "own": striped(np.random.randint(0, S, U)),
    }


def reference(xT, w1, res, offs, own):
    xq = mxq(f64(xT)[:, unstriped(offs)], 0, "e4m3")
    y = relu(mxq(f64(w1), 0, "e4m3").T @ xq)
    return f64(res) + y[:, unstriped(own)]

@@ -1,0 +1,110 @@
+from contextlib import ExitStack
+
+import concourse.mybir as mybir
+
+K, T, S, N, U = 512, 2048, 1024, 128, 2048
+FLOPS = 2 * K * N * S
+
+F32 = mybir.dt.float32
+BF16 = mybir.dt.bfloat16
+U32 = mybir.dt.uint32
+U16 = mybir.dt.uint16
+U8 = mybir.dt.uint8
+FP8X4 = mybir.dt.float8_e4m3fn_x4
+COPY = mybir.ActivationFunctionType.Copy
+RELU = mybir.ActivationFunctionType.Relu
+ADD = mybir.AluOpType.add
+
+P = 128
+PACK = 4
+LIST_ROWS = 16
+
+VECTOR_GROUPS = [(0, 384)]
+SCALAR_GROUPS = [(384, 768), (768, 1024)]
+PLANE_CHUNKS = [[1024, 1024], [1024, 1024], [1024, 1024], [1024, 512, 512]]
+OUT_PIECES = [512, 512, 512, 256, 128, 128]
+
+
+def spans(widths):
+    edges = [sum(widths[:i]) for i in range(len(widths) + 1)]
+    return [(edges[i], edges[i + 1]) for i in range(len(widths))]
+
+
+def entries(lst, lo, hi):
+    return lst[:, lo // LIST_ROWS : hi // LIST_ROWS]
+
+
+def tile_picked_unmerge_relu_e_kernel(tc, xT, w1, res, offs, own, out):
+    nc = tc.nc
+    x_rows = xT.rearrange("(p j) t -> p j t", j=PACK)
+
+    with ExitStack() as ctx:
+        lists = ctx.enter_context(tc.tile_pool(name="lists", bufs=1))
+        keep = ctx.enter_context(tc.tile_pool(name="keep", bufs=1))
+        psum = ctx.enter_context(tc.psum_pool(name="psum", bufs=1))
+
+        offs_sb = lists.tile([P, S // LIST_ROWS], U16, name="offs_sb")
+        own_sb = lists.tile([P, U // LIST_ROWS], U16, name="own_sb")
+
+        w_raw = keep.tile([P, PACK, N], F32, name="w_raw")
+        nc.sync.dma_start(out=w_raw[:], in_=w1.rearrange("(p j) n -> p j n", j=PACK))
+        planes = [keep.tile([P, T], F32, name="plane%d" % j) for j in range(PACK)]
+        rounded = [keep.tile([P, T], BF16, name="rounded%d" % j) for j in range(PACK)]
+        for j in range(PACK):
+            for c, (lo, hi) in enumerate(spans(PLANE_CHUNKS[j])):
+                nc.sync.dma_start(out=planes[j][:, lo:hi], in_=x_rows[:, j, lo:hi])
+                if j == 0 and c == 0:
+                    nc.sync.dma_start(offs_sb[:], offs)
+        nc.sync.dma_start(own_sb[:], own)
+        res_sb = keep.tile([P, U], F32, name="res_sb")
+        for lo, hi in spans([U // 2, U // 2]):
+            nc.sync.dma_start(out=res_sb[:, lo:hi], in_=res[:, lo:hi])
+
+        w_grouped = keep.tile([P, N, PACK], BF16, name="w_grouped", align_bytes=64)
+        nc.scalar.activation(w_grouped[:], w_raw[:].rearrange("p j n -> p n j"), COPY)
+        w_codes = keep.tile([P, N], U32, name="w_codes", align_bytes=64)
+        w_scales = keep.tile([P, N], U8, name="w_scales", align_bytes=64)
+        nc.vector.quantize_mx(
+            out=w_codes[:].bitcast(FP8X4), scales=w_scales[:], in_=w_grouped[:].rearrange("p n j -> p (n j)")
+        )
+
+        grouped = {}
+        for lo, hi in VECTOR_GROUPS + SCALAR_GROUPS:
+            grouped[lo] = keep.tile([P, hi - lo, PACK], BF16, name="grouped%d" % lo, align_bytes=64)
+        for j in range(PACK):
+            for lo, hi in spans(PLANE_CHUNKS[j]):
+                nc.vector.tensor_copy(out=rounded[j][:, lo:hi], in_=planes[j][:, lo:hi])
+            for lo, hi in SCALAR_GROUPS:
+                nc.scalar.activation(grouped[lo][:, :, j], rounded[j][:].indirect(entries(offs_sb, lo, hi)), COPY)
+            for lo, hi in VECTOR_GROUPS:
+                nc.vector.tensor_copy(out=grouped[lo][:, :, j], in_=planes[j][:].indirect(entries(offs_sb, lo, hi)))
+
+        y = keep.tile([P, S], F32, name="y")
+        PRODUCTS = [(384, 384, 640, "s"), (0, 0, 256, "s"), (384, 640, 768, "s"), (0, 256, 384, "s"), (768, 768, 1024, "v")]
+        for base, lo, hi, engine in PRODUCTS:
+            codes = keep.tile([P, hi - lo], U32, name="codes%d" % lo, align_bytes=64)
+            scales = keep.tile([P, hi - lo], U8, name="scales%d" % lo, align_bytes=64)
+            nc.vector.quantize_mx(
+                out=codes[:].bitcast(FP8X4),
+                scales=scales[:],
+                in_=grouped[base][:, lo - base : hi - base, :].rearrange("p n j -> p (n j)"),
+            )
+            acc = psum.tile([P, hi - lo], F32, name="acc%d" % lo)
+            nc.tensor.matmul_mx(
+                out=acc[:],
+                lhsT=w_codes[:].bitcast(FP8X4),
+                lhsT_scale=w_scales[:],
+                rhs=codes[:].bitcast(FP8X4),
+                rhs_scale=scales[:],
+                start=True,
+                stop=True,
+            )
+            if engine == "s":
+                nc.scalar.activation(y[:, lo:hi], acc[:], RELU)
+            else:
+                nc.vector.tensor_scalar_max(y[:, lo:hi], acc[:], 0.0)
+
+        for lo, hi in spans(OUT_PIECES):
+            result = keep.tile([P, hi - lo], F32, name="result%d" % lo)
+            nc.vector.tensor_tensor(result[:], y[:].indirect(entries(own_sb, lo, hi)), res_sb[:, lo:hi], ADD)
+            nc.sync.dma_start(out=out[:, lo:hi], in_=result[:])

@@ -18,10 +18,13 @@ ADD = mybir.AluOpType.add
 P = 128
 PACK = 4
 LIST_ROWS = 16
+W_RAW_BYTES = PACK * N * 4
 
-VECTOR_GROUPS = [(0, 384)]
-SCALAR_GROUPS = [(384, 768), (768, 1024)]
-PLANE_CHUNKS = [[1024, 1024], [1024, 1024], [1024, 1024], [1024, 512, 512]]
+VECTOR_GROUPS = [(0, 352)]
+SCALAR_GROUPS = [(352, 768), (768, 1024)]
+PLANE_CHUNKS = [[1536, 512], [1280, 512, 256], [1280, 512, 256], [1280, 512, 256]]
+FIRST_PLANE_ROUNDING = [(0, 1024, "v"), (1024, 1536, "s"), (1536, 1888, "v"), (1888, 2048, "s")]
+PRODUCTS = [(0, 256, "s"), (256, 512, "s"), (512, 768, "v"), (768, 896, "s"), (896, 1024, "v")]
 OUT_PIECES = [512, 512, 512, 256, 128, 128]
 
 
@@ -41,13 +44,12 @@ def tile_picked_unmerge_relu_e_kernel(tc, xT, w1, res, offs, own, out):
     with ExitStack() as ctx:
         lists = ctx.enter_context(tc.tile_pool(name="lists", bufs=1))
         keep = ctx.enter_context(tc.tile_pool(name="keep", bufs=1))
+        reused = ctx.enter_context(tc.tile_pool(name="reused", bufs=1))
         psum = ctx.enter_context(tc.psum_pool(name="psum", bufs=1))
 
         offs_sb = lists.tile([P, S // LIST_ROWS], U16, name="offs_sb")
         own_sb = lists.tile([P, U // LIST_ROWS], U16, name="own_sb")
 
-        w_raw = keep.tile([P, PACK, N], F32, name="w_raw")
-        nc.sync.dma_start(out=w_raw[:], in_=w1.rearrange("(p j) n -> p j n", j=PACK))
         planes = [keep.tile([P, T], F32, name="plane%d" % j) for j in range(PACK)]
         rounded = [keep.tile([P, T], BF16, name="rounded%d" % j) for j in range(PACK)]
         for j in range(PACK):
@@ -55,39 +57,43 @@ def tile_picked_unmerge_relu_e_kernel(tc, xT, w1, res, offs, own, out):
                 nc.sync.dma_start(out=planes[j][:, lo:hi], in_=x_rows[:, j, lo:hi])
                 if j == 0 and c == 0:
                     nc.sync.dma_start(offs_sb[:], offs)
+        w_raw = reused.tile([P, PACK, N], F32, name="w_raw", align_bytes=64, offset=0)
+        nc.sync.dma_start(out=w_raw[:], in_=w1.rearrange("(p j) n -> p j n", j=PACK))
         nc.sync.dma_start(own_sb[:], own)
         res_sb = keep.tile([P, U], F32, name="res_sb")
-        for lo, hi in spans([U // 2, U // 2]):
-            nc.sync.dma_start(out=res_sb[:, lo:hi], in_=res[:, lo:hi])
+        nc.sync.dma_start(out=res_sb[:], in_=res)
 
-        w_grouped = keep.tile([P, N, PACK], BF16, name="w_grouped", align_bytes=64)
-        nc.scalar.activation(w_grouped[:], w_raw[:].rearrange("p j n -> p n j"), COPY)
+        grouped = keep.tile([P, S * PACK], BF16, name="grouped", align_bytes=64)
+        slots = grouped[:].rearrange("p (n j) -> p n j", j=PACK)
+        for j in range(PACK):
+            rounding = FIRST_PLANE_ROUNDING if j == 0 else [(lo, hi, "v") for lo, hi in spans(PLANE_CHUNKS[j])]
+            for lo, hi, engine in rounding:
+                if engine == "s":
+                    nc.scalar.activation(rounded[j][:, lo:hi], planes[j][:, lo:hi], COPY)
+                else:
+                    nc.vector.tensor_copy(out=rounded[j][:, lo:hi], in_=planes[j][:, lo:hi])
+            for lo, hi in SCALAR_GROUPS:
+                nc.scalar.activation(slots[:, lo:hi, j], rounded[j][:].indirect(entries(offs_sb, lo, hi)), COPY)
+            for lo, hi in VECTOR_GROUPS:
+                nc.vector.tensor_copy(out=slots[:, lo:hi, j], in_=planes[j][:].indirect(entries(offs_sb, lo, hi)))
+
+        w_grouped = reused.tile([P, N, PACK], BF16, name="w_grouped", align_bytes=64, offset=W_RAW_BYTES)
+        nc.vector.tensor_copy(out=w_grouped[:], in_=w_raw[:].rearrange("p j n -> p n j"))
         w_codes = keep.tile([P, N], U32, name="w_codes", align_bytes=64)
         w_scales = keep.tile([P, N], U8, name="w_scales", align_bytes=64)
         nc.vector.quantize_mx(
             out=w_codes[:].bitcast(FP8X4), scales=w_scales[:], in_=w_grouped[:].rearrange("p n j -> p (n j)")
         )
 
-        grouped = {}
-        for lo, hi in VECTOR_GROUPS + SCALAR_GROUPS:
-            grouped[lo] = keep.tile([P, hi - lo, PACK], BF16, name="grouped%d" % lo, align_bytes=64)
-        for j in range(PACK):
-            for lo, hi in spans(PLANE_CHUNKS[j]):
-                nc.vector.tensor_copy(out=rounded[j][:, lo:hi], in_=planes[j][:, lo:hi])
-            for lo, hi in SCALAR_GROUPS:
-                nc.scalar.activation(grouped[lo][:, :, j], rounded[j][:].indirect(entries(offs_sb, lo, hi)), COPY)
-            for lo, hi in VECTOR_GROUPS:
-                nc.vector.tensor_copy(out=grouped[lo][:, :, j], in_=planes[j][:].indirect(entries(offs_sb, lo, hi)))
-
         y = keep.tile([P, S], F32, name="y")
-        PRODUCTS = [(384, 384, 640, "s"), (0, 0, 256, "s"), (384, 640, 768, "s"), (0, 256, 384, "s"), (768, 768, 1024, "v")]
-        for base, lo, hi, engine in PRODUCTS:
+        for lo, hi, engine in PRODUCTS:
             codes = keep.tile([P, hi - lo], U32, name="codes%d" % lo, align_bytes=64)
-            scales = keep.tile([P, hi - lo], U8, name="scales%d" % lo, align_bytes=64)
+            place = 0 if lo == 0 else W_RAW_BYTES + lo - 256
+            scales = reused.tile([P, hi - lo], U8, name="scales%d" % lo, align_bytes=64, offset=place)
             nc.vector.quantize_mx(
                 out=codes[:].bitcast(FP8X4),
                 scales=scales[:],
-                in_=grouped[base][:, lo - base : hi - base, :].rearrange("p n j -> p (n j)"),
+                in_=grouped[:, PACK * lo : PACK * hi],
             )
             acc = psum.tile([P, hi - lo], F32, name="acc%d" % lo)
             nc.tensor.matmul_mx(

@@ -20,12 +20,12 @@ PACK = 4
 LIST_ROWS = 16
 W_RAW_BYTES = PACK * N * 4
 
-VECTOR_GROUPS = [(0, 352)]
-SCALAR_GROUPS = [(352, 768), (768, 1024)]
-PLANE_CHUNKS = [[1536, 512], [1280, 512, 256], [1280, 512, 256], [1280, 512, 256]]
+VECTOR_GROUPS = [(0, 384)]
+SCALAR_GROUPS = [(384, 768), (768, 1024)]
+PLANE_CHUNKS = [[1536, 512], [768, 768, 512], [768, 768, 512], [768, 768, 256, 256]]
 FIRST_PLANE_ROUNDING = [(0, 1024, "v"), (1024, 1536, "s"), (1536, 1888, "v"), (1888, 2048, "s")]
 PRODUCTS = [(0, 256, "s"), (256, 512, "s"), (512, 768, "v"), (768, 896, "s"), (896, 1024, "v")]
-OUT_PIECES = [512, 512, 512, 256, 128, 128]
+OUT_PIECES = [768, 640, 384, 128, 128]
 
 
 def spans(widths):
@@ -66,13 +66,15 @@ def tile_picked_unmerge_relu_e_kernel(tc, xT, w1, res, offs, own, out):
         grouped = keep.tile([P, S * PACK], BF16, name="grouped", align_bytes=64)
         slots = grouped[:].rearrange("p (n j) -> p n j", j=PACK)
         for j in range(PACK):
-            rounding = FIRST_PLANE_ROUNDING if j == 0 else [(lo, hi, "v") for lo, hi in spans(PLANE_CHUNKS[j])]
+            rounding = FIRST_PLANE_ROUNDING if j == 0 else [(lo, hi, "g" if lo == 0 else "v") for lo, hi in spans(PLANE_CHUNKS[j])]
             for lo, hi, engine in rounding:
                 if engine == "s":
                     nc.scalar.activation(rounded[j][:, lo:hi], planes[j][:, lo:hi], COPY)
+                elif engine == "g":
+                    nc.gpsimd.tensor_copy(out=rounded[j][:, lo:hi], in_=planes[j][:, lo:hi])
                 else:
                     nc.vector.tensor_copy(out=rounded[j][:, lo:hi], in_=planes[j][:, lo:hi])
-            for lo, hi in SCALAR_GROUPS:
+            for lo, hi in SCALAR_GROUPS if j == PACK - 1 else [(SCALAR_GROUPS[0][0], S)]:
                 nc.scalar.activation(slots[:, lo:hi, j], rounded[j][:].indirect(entries(offs_sb, lo, hi)), COPY)
             for lo, hi in VECTOR_GROUPS:
                 nc.vector.tensor_copy(out=slots[:, lo:hi, j], in_=planes[j][:].indirect(entries(offs_sb, lo, hi)))

@@ -20,12 +20,15 @@ PACK = 4
 LIST_ROWS = 16
 W_RAW_BYTES = PACK * N * 4
 
-VECTOR_GROUPS = [(0, 384)]
-SCALAR_GROUPS = [(384, 768), (768, 1024)]
-PLANE_CHUNKS = [[1536, 512], [768, 768, 512], [768, 768, 512], [768, 768, 256, 256]]
-FIRST_PLANE_ROUNDING = [(0, 1024, "v"), (1024, 1536, "s"), (1536, 1888, "v"), (1888, 2048, "s")]
-PRODUCTS = [(0, 256, "s"), (256, 512, "s"), (512, 768, "v"), (768, 896, "s"), (896, 1024, "v")]
-OUT_PIECES = [768, 640, 384, 128, 128]
+PLANES = [
+    (0, [1536, 512], [(0, 1024, "v"), (1024, 1536, "s"), (1536, 1888, "v"), (1888, 2048, "s")], [(384, 1024, "s"), (0, 384, "v")]),
+    (1, [768, 768, 512], [(0, 768, "g"), (768, 1536, "v"), (1536, 2048, "v")], [(384, 1024, "s"), (0, 384, "v")]),
+    (2, [768, 768, 512], [(0, 768, "g"), (768, 1536, "v"), (1536, 2048, "v")], [(384, 1024, "s"), (0, 384, "v")]),
+    (3, [768, 768, 256, 256], [(0, 768, "g"), (768, 1536, "v"), (1536, 1792, "v"), (1792, 2048, "v")], [(384, 768, "s"), (768, 1024, "s"), (0, 384, "v")]),
+]
+PRODUCTS = [(0, 256, "s"), (256, 512, "s"), (512, 768, "v"), (768, 896, "s"), (896, 960, "v"), (960, 1024, "v")]
+OUT_PIECES = [608, 736, 384, 192, 128]
+RES_PIECES = [2048]
 
 
 def spans(widths):
@@ -50,23 +53,23 @@ def tile_picked_unmerge_relu_e_kernel(tc, xT, w1, res, offs, own, out):
         offs_sb = lists.tile([P, S // LIST_ROWS], U16, name="offs_sb")
         own_sb = lists.tile([P, U // LIST_ROWS], U16, name="own_sb")
 
-        planes = [keep.tile([P, T], F32, name="plane%d" % j) for j in range(PACK)]
-        rounded = [keep.tile([P, T], BF16, name="rounded%d" % j) for j in range(PACK)]
-        for j in range(PACK):
-            for c, (lo, hi) in enumerate(spans(PLANE_CHUNKS[j])):
+        planes = {j: keep.tile([P, T], F32, name="plane%d" % j) for j in range(PACK)}
+        rounded = {j: keep.tile([P, T], BF16, name="rounded%d" % j) for j, loads, rounding, gathers in PLANES if rounding}
+        for n, (j, loads, rounding, gathers) in enumerate(PLANES):
+            for c, (lo, hi) in enumerate(spans(loads)):
                 nc.sync.dma_start(out=planes[j][:, lo:hi], in_=x_rows[:, j, lo:hi])
-                if j == 0 and c == 0:
+                if n == 0 and c == 0:
                     nc.sync.dma_start(offs_sb[:], offs)
         w_raw = reused.tile([P, PACK, N], F32, name="w_raw", align_bytes=64, offset=0)
         nc.sync.dma_start(out=w_raw[:], in_=w1.rearrange("(p j) n -> p j n", j=PACK))
         nc.sync.dma_start(own_sb[:], own)
         res_sb = keep.tile([P, U], F32, name="res_sb")
-        nc.sync.dma_start(out=res_sb[:], in_=res)
+        for lo, hi in spans(RES_PIECES):
+            nc.sync.dma_start(out=res_sb[:, lo:hi], in_=res[:, lo:hi])
 
         grouped = keep.tile([P, S * PACK], BF16, name="grouped", align_bytes=64)
         slots = grouped[:].rearrange("p (n j) -> p n j", j=PACK)
-        for j in range(PACK):
-            rounding = FIRST_PLANE_ROUNDING if j == 0 else [(lo, hi, "g" if lo == 0 else "v") for lo, hi in spans(PLANE_CHUNKS[j])]
+        for j, loads, rounding, gathers in PLANES:
             for lo, hi, engine in rounding:
                 if engine == "s":
                     nc.scalar.activation(rounded[j][:, lo:hi], planes[j][:, lo:hi], COPY)
@@ -74,13 +77,14 @@ def tile_picked_unmerge_relu_e_kernel(tc, xT, w1, res, offs, own, out):
                     nc.gpsimd.tensor_copy(out=rounded[j][:, lo:hi], in_=planes[j][:, lo:hi])
                 else:
                     nc.vector.tensor_copy(out=rounded[j][:, lo:hi], in_=planes[j][:, lo:hi])
-            for lo, hi in SCALAR_GROUPS if j == PACK - 1 else [(SCALAR_GROUPS[0][0], S)]:
-                nc.scalar.activation(slots[:, lo:hi, j], rounded[j][:].indirect(entries(offs_sb, lo, hi)), COPY)
-            for lo, hi in VECTOR_GROUPS:
-                nc.vector.tensor_copy(out=slots[:, lo:hi, j], in_=planes[j][:].indirect(entries(offs_sb, lo, hi)))
+            for lo, hi, engine in gathers:
+                if engine == "s":
+                    nc.scalar.activation(slots[:, lo:hi, j], rounded[j][:].indirect(entries(offs_sb, lo, hi)), COPY)
+                else:
+                    nc.vector.tensor_copy(out=slots[:, lo:hi, j], in_=planes[j][:].indirect(entries(offs_sb, lo, hi)))
 
         w_grouped = reused.tile([P, N, PACK], BF16, name="w_grouped", align_bytes=64, offset=W_RAW_BYTES)
-        nc.vector.tensor_copy(out=w_grouped[:], in_=w_raw[:].rearrange("p j n -> p n j"))
+        nc.gpsimd.tensor_copy(out=w_grouped[:], in_=w_raw[:].rearrange("p j n -> p n j"))
         w_codes = keep.tile([P, N], U32, name="w_codes", align_bytes=64)
         w_scales = keep.tile([P, N], U8, name="w_scales", align_bytes=64)
         nc.vector.quantize_mx(
@@ -90,7 +94,7 @@ def tile_picked_unmerge_relu_e_kernel(tc, xT, w1, res, offs, own, out):
         y = keep.tile([P, S], F32, name="y")
         for lo, hi, engine in PRODUCTS:
             codes = keep.tile([P, hi - lo], U32, name="codes%d" % lo, align_bytes=64)
-            place = 0 if lo == 0 else W_RAW_BYTES + lo - 256
+            place = 2 * W_RAW_BYTES if lo == 0 else lo
             scales = reused.tile([P, hi - lo], U8, name="scales%d" % lo, align_bytes=64, offset=place)
             nc.vector.quantize_mx(
                 out=codes[:].bitcast(FP8X4),

@@ -21,12 +21,12 @@ LIST_ROWS = 16
 W_RAW_BYTES = PACK * N * 4
 
 PLANES = [
-    (0, [1536, 512], [(0, 1024, "v"), (1024, 1536, "s"), (1536, 1888, "v"), (1888, 2048, "s")], [(384, 1024, "s"), (0, 384, "v")]),
-    (1, [768, 768, 512], [(0, 768, "g"), (768, 1536, "v"), (1536, 2048, "v")], [(384, 1024, "s"), (0, 384, "v")]),
-    (2, [768, 768, 512], [(0, 768, "g"), (768, 1536, "v"), (1536, 2048, "v")], [(384, 1024, "s"), (0, 384, "v")]),
-    (3, [768, 768, 256, 256], [(0, 768, "g"), (768, 1536, "v"), (1536, 1792, "v"), (1792, 2048, "v")], [(384, 768, "s"), (768, 1024, "s"), (0, 384, "v")]),
+    (0, [1536, 512], [(0, 1024, "v"), (1024, 1536, "s"), (1536, 1888, "v"), (1888, 2048, "s")], [(416, 1024, "s"), (0, 416, "v")]),
+    (1, [768, 768, 512], [(0, 768, "g"), (768, 1536, "v"), (1536, 2048, "v")], [(416, 1024, "s"), (0, 416, "v")]),
+    (2, [768, 768, 512], [(0, 768, "g"), (768, 1536, "v"), (1536, 2048, "v")], [(416, 1024, "s"), (0, 416, "v")]),
+    (3, [768, 768, 256, 256], [(0, 768, "g"), (768, 1536, "v"), (1536, 1792, "v"), (1792, 2048, "v")], [(416, 768, "s"), (768, 1024, "s"), (0, 416, "v")]),
 ]
-PRODUCTS = [(0, 256, "s"), (256, 512, "s"), (512, 768, "v"), (768, 896, "s"), (896, 960, "v"), (960, 1024, "v")]
+PRODUCTS = [(0, 256, "s"), (256, 512, "s"), (512, 768, "v"), (768, 896, "s"), (896, 1024, "v")]
 OUT_PIECES = [608, 736, 384, 192, 128]
 RES_PIECES = [2048]
 
@@ -56,10 +56,10 @@ def tile_picked_unmerge_relu_e_kernel(tc, xT, w1, res, offs, own, out):
         planes = {j: keep.tile([P, T], F32, name="plane%d" % j) for j in range(PACK)}
         rounded = {j: keep.tile([P, T], BF16, name="rounded%d" % j) for j, loads, rounding, gathers in PLANES if rounding}
         for n, (j, loads, rounding, gathers) in enumerate(PLANES):
-            for c, (lo, hi) in enumerate(spans(loads)):
+            for lo, hi in spans(loads):
                 nc.sync.dma_start(out=planes[j][:, lo:hi], in_=x_rows[:, j, lo:hi])
-                if n == 0 and c == 0:
-                    nc.sync.dma_start(offs_sb[:], offs)
+            if n == 0:
+                nc.sync.dma_start(offs_sb[:], offs)
         w_raw = reused.tile([P, PACK, N], F32, name="w_raw", align_bytes=64, offset=0)
         nc.sync.dma_start(out=w_raw[:], in_=w1.rearrange("(p j) n -> p j n", j=PACK))
         nc.sync.dma_start(own_sb[:], own)
@@ -94,8 +94,7 @@ def tile_picked_unmerge_relu_e_kernel(tc, xT, w1, res, offs, own, out):
         y = keep.tile([P, S], F32, name="y")
         for lo, hi, engine in PRODUCTS:
             codes = keep.tile([P, hi - lo], U32, name="codes%d" % lo, align_bytes=64)
-            place = 2 * W_RAW_BYTES if lo == 0 else lo
-            scales = reused.tile([P, hi - lo], U8, name="scales%d" % lo, align_bytes=64, offset=place)
+            scales = reused.tile([P, hi - lo], U8, name="scales%d" % lo, align_bytes=64, offset=lo)
             nc.vector.quantize_mx(
                 out=codes[:].bitcast(FP8X4),
                 scales=scales[:],

@@ -23,8 +23,8 @@ W_RAW_BYTES = PACK * N * 4
 PLANES = [
     (0, [1536, 512], [(0, 1024, "v"), (1024, 1536, "s"), (1536, 1888, "v"), (1888, 2048, "s")], [(416, 1024, "s"), (0, 416, "v")]),
     (1, [768, 768, 512], [(0, 768, "g"), (768, 1536, "v"), (1536, 2048, "v")], [(416, 1024, "s"), (0, 416, "v")]),
-    (2, [768, 768, 512], [(0, 768, "g"), (768, 1536, "v"), (1536, 2048, "v")], [(416, 1024, "s"), (0, 416, "v")]),
-    (3, [768, 768, 256, 256], [(0, 768, "g"), (768, 1536, "v"), (1536, 1792, "v"), (1792, 2048, "v")], [(416, 768, "s"), (768, 1024, "s"), (0, 416, "v")]),
+    (2, [768, 768, 256, 256], [(0, 768, "g"), (768, 1536, "v"), (1536, 1792, "v"), (1792, 2048, "v")], [(416, 1024, "s"), (0, 416, "v")]),
+    (3, [768, 768, 256, 128, 128], [(0, 768, "g"), (768, 1536, "v"), (1536, 1792, "v"), (1792, 1920, "v"), (1920, 2048, "v")], [(416, 768, "s"), (768, 1024, "s"), (0, 416, "v")]),
 ]
 PRODUCTS = [(0, 256, "s"), (256, 512, "s"), (512, 768, "v"), (768, 896, "s"), (896, 1024, "v")]
 OUT_PIECES = [608, 736, 384, 192, 128]

@@ -20,15 +20,16 @@ PACK = 4
 LIST_ROWS = 16
 W_RAW_BYTES = PACK * N * 4
 
-PLANES = [
-    (0, [1536, 512], [(0, 1024, "v"), (1024, 1536, "s"), (1536, 1888, "v"), (1888, 2048, "s")], [(416, 1024, "s"), (0, 416, "v")]),
-    (1, [768, 768, 512], [(0, 768, "g"), (768, 1536, "v"), (1536, 2048, "v")], [(416, 1024, "s"), (0, 416, "v")]),
-    (2, [768, 768, 256, 256], [(0, 768, "g"), (768, 1536, "v"), (1536, 1792, "v"), (1792, 2048, "v")], [(416, 1024, "s"), (0, 416, "v")]),
-    (3, [768, 768, 256, 128, 128], [(0, 768, "g"), (768, 1536, "v"), (1536, 1792, "v"), (1792, 1920, "v"), (1920, 2048, "v")], [(416, 768, "s"), (768, 1024, "s"), (0, 416, "v")]),
-]
-PRODUCTS = [(0, 256, "s"), (256, 512, "s"), (512, 768, "v"), (768, 896, "s"), (896, 1024, "v")]
+VECTOR_ENTRIES = 416
+LAST_GATHER = T // 8
+
+FIRST_PLANE_LOADS = [1536, 512]
+FIRST_PLANE_ROUNDING = [(0, 1024, "vector"), (1024, 1536, "scalar"), (1536, 1888, "vector"), (1888, 2048, "scalar")]
+LATER_PLANE_LOADS = [640, 768, 384, 256]
+
+STRETCH = 128
+BANKS = [(0, 256, "scalar"), (256, 512, "scalar"), (512, 768, "vector"), (768, 896, "scalar"), (896, 1024, "vector")]
 OUT_PIECES = [608, 736, 384, 192, 128]
-RES_PIECES = [2048]
 
 
 def spans(widths):
@@ -36,8 +37,8 @@ def spans(widths):
     return [(edges[i], edges[i + 1]) for i in range(len(widths))]
 
 
-def entries(lst, lo, hi):
-    return lst[:, lo // LIST_ROWS : hi // LIST_ROWS]
+def entries(list_tile, lo, hi):
+    return list_tile[:, lo // LIST_ROWS : hi // LIST_ROWS]
 
 
 def tile_picked_unmerge_relu_e_kernel(tc, xT, w1, res, offs, own, out):
@@ -53,35 +54,39 @@ def tile_picked_unmerge_relu_e_kernel(tc, xT, w1, res, offs, own, out):
         offs_sb = lists.tile([P, S // LIST_ROWS], U16, name="offs_sb")
         own_sb = lists.tile([P, U // LIST_ROWS], U16, name="own_sb")
 
-        planes = {j: keep.tile([P, T], F32, name="plane%d" % j) for j in range(PACK)}
-        rounded = {j: keep.tile([P, T], BF16, name="rounded%d" % j) for j, loads, rounding, gathers in PLANES if rounding}
-        for n, (j, loads, rounding, gathers) in enumerate(PLANES):
-            for lo, hi in spans(loads):
+        planes = [keep.tile([P, T], F32, name="plane%d" % j) for j in range(PACK)]
+        rounded = [keep.tile([P, T], BF16, name="rounded%d" % j) for j in range(PACK)]
+        for j in range(PACK):
+            for lo, hi in spans(FIRST_PLANE_LOADS if j == 0 else LATER_PLANE_LOADS):
                 nc.sync.dma_start(out=planes[j][:, lo:hi], in_=x_rows[:, j, lo:hi])
-            if n == 0:
+            if j == 0:
                 nc.sync.dma_start(offs_sb[:], offs)
         w_raw = reused.tile([P, PACK, N], F32, name="w_raw", align_bytes=64, offset=0)
         nc.sync.dma_start(out=w_raw[:], in_=w1.rearrange("(p j) n -> p j n", j=PACK))
         nc.sync.dma_start(own_sb[:], own)
         res_sb = keep.tile([P, U], F32, name="res_sb")
-        for lo, hi in spans(RES_PIECES):
-            nc.sync.dma_start(out=res_sb[:, lo:hi], in_=res[:, lo:hi])
+        nc.sync.dma_start(out=res_sb[:, 0:U], in_=res[:, 0:U])
 
         grouped = keep.tile([P, S * PACK], BF16, name="grouped", align_bytes=64)
-        slots = grouped[:].rearrange("p (n j) -> p n j", j=PACK)
-        for j, loads, rounding, gathers in PLANES:
-            for lo, hi, engine in rounding:
-                if engine == "s":
+        places = grouped[:].rearrange("p (e j) -> p e j", j=PACK)
+        later_rounding = [(lo, hi, "gpsimd" if lo == 0 else "vector") for lo, hi in spans(LATER_PLANE_LOADS)]
+        for j in range(PACK):
+            for lo, hi, engine in FIRST_PLANE_ROUNDING if j == 0 else later_rounding:
+                if engine == "scalar":
                     nc.scalar.activation(rounded[j][:, lo:hi], planes[j][:, lo:hi], COPY)
-                elif engine == "g":
+                elif engine == "gpsimd":
                     nc.gpsimd.tensor_copy(out=rounded[j][:, lo:hi], in_=planes[j][:, lo:hi])
                 else:
                     nc.vector.tensor_copy(out=rounded[j][:, lo:hi], in_=planes[j][:, lo:hi])
-            for lo, hi, engine in gathers:
-                if engine == "s":
-                    nc.scalar.activation(slots[:, lo:hi, j], rounded[j][:].indirect(entries(offs_sb, lo, hi)), COPY)
-                else:
-                    nc.vector.tensor_copy(out=slots[:, lo:hi, j], in_=planes[j][:].indirect(entries(offs_sb, lo, hi)))
+            if j == PACK - 1:
+                scalar_gathers = [(VECTOR_ENTRIES, S - LAST_GATHER), (S - LAST_GATHER, S)]
+            else:
+                scalar_gathers = [(VECTOR_ENTRIES, S)]
+            for lo, hi in scalar_gathers:
+                nc.scalar.activation(places[:, lo:hi, j], rounded[j][:].indirect(entries(offs_sb, lo, hi)), COPY)
+            nc.vector.tensor_copy(
+                out=places[:, 0:VECTOR_ENTRIES, j], in_=planes[j][:].indirect(entries(offs_sb, 0, VECTOR_ENTRIES))
+            )
 
         w_grouped = reused.tile([P, N, PACK], BF16, name="w_grouped", align_bytes=64, offset=W_RAW_BYTES)
         nc.gpsimd.tensor_copy(out=w_grouped[:], in_=w_raw[:].rearrange("p j n -> p n j"))
@@ -92,25 +97,26 @@ def tile_picked_unmerge_relu_e_kernel(tc, xT, w1, res, offs, own, out):
         )
 
         y = keep.tile([P, S], F32, name="y")
-        for lo, hi, engine in PRODUCTS:
-            codes = keep.tile([P, hi - lo], U32, name="codes%d" % lo, align_bytes=64)
-            scales = reused.tile([P, hi - lo], U8, name="scales%d" % lo, align_bytes=64, offset=lo)
-            nc.vector.quantize_mx(
-                out=codes[:].bitcast(FP8X4),
-                scales=scales[:],
-                in_=grouped[:, PACK * lo : PACK * hi],
-            )
+        for lo, hi, engine in BANKS:
             acc = psum.tile([P, hi - lo], F32, name="acc%d" % lo)
-            nc.tensor.matmul_mx(
-                out=acc[:],
-                lhsT=w_codes[:].bitcast(FP8X4),
-                lhsT_scale=w_scales[:],
-                rhs=codes[:].bitcast(FP8X4),
-                rhs_scale=scales[:],
-                start=True,
-                stop=True,
-            )
-            if engine == "s":
+            for first in range(lo, hi, STRETCH):
+                codes = keep.tile([P, STRETCH], U32, name="codes%d" % first, align_bytes=64)
+                scales = reused.tile([P, STRETCH], U8, name="scales%d" % first, align_bytes=64, offset=first)
+                nc.vector.quantize_mx(
+                    out=codes[:].bitcast(FP8X4),
+                    scales=scales[:],
+                    in_=grouped[:, PACK * first : PACK * (first + STRETCH)],
+                )
+                nc.tensor.matmul_mx(
+                    out=acc[:, first - lo : first - lo + STRETCH],
+                    lhsT=w_codes[:].bitcast(FP8X4),
+                    lhsT_scale=w_scales[:],
+                    rhs=codes[:].bitcast(FP8X4),
+                    rhs_scale=scales[:],
+                    start=True,
+                    stop=True,
+                )
+            if engine == "scalar":
                 nc.scalar.activation(y[:, lo:hi], acc[:], RELU)
             else:
                 nc.vector.tensor_scalar_max(y[:, lo:hi], acc[:], 0.0)

@@ -20,15 +20,18 @@ PACK = 4
 LIST_ROWS = 16
 W_RAW_BYTES = PACK * N * 4
 
-VECTOR_ENTRIES = 416
+VECTOR_ENTRIES = [416,416,416,416]
 LAST_GATHER = T // 8
-
-FIRST_PLANE_LOADS = [1536, 512]
-FIRST_PLANE_ROUNDING = [(0, 1024, "vector"), (1024, 1536, "scalar"), (1536, 1888, "vector"), (1888, 2048, "scalar")]
-LATER_PLANE_LOADS = [640, 768, 384, 256]
+PLANE_LOADS = [[1536,512],[640,768,384,256],[640,768,384,256],[640,768,384,256]]
+ROUNDING = [
+    [(0, 1024, "vector"), (1024, 1536, "scalar"), (1536, 1888, "vector"), (1888, 2048, "scalar")],
+    [(0, 640, "gpsimd"), (640, 1408, "vector"), (1408, 1792, "vector"), (1792, 2048, "vector")],
+    [(0, 640, "gpsimd"), (640, 1408, "vector"), (1408, 1792, "vector"), (1792, 2048, "vector")],
+    [(0, 640, "gpsimd"), (640, 1408, "vector"), (1408, 1792, "vector"), (1792, 2048, "vector")],
+]
 
 STRETCH = 128
-BANKS = [(0, 256, "scalar"), (256, 512, "scalar"), (512, 768, "vector"), (768, 896, "scalar"), (896, 1024, "vector")]
+BANKS = [(0, 256, "scalar"), (256, 512, "scalar"), (512, 768, "vector"), (768, 896, "scalar"), (896, 1024, "scalar")]
 OUT_PIECES = [608, 736, 384, 192, 128]
 
 
@@ -57,7 +60,7 @@ def tile_picked_unmerge_relu_e_kernel(tc, xT, w1, res, offs, own, out):
         planes = [keep.tile([P, T], F32, name="plane%d" % j) for j in range(PACK)]
         rounded = [keep.tile([P, T], BF16, name="rounded%d" % j) for j in range(PACK)]
         for j in range(PACK):
-            for lo, hi in spans(FIRST_PLANE_LOADS if j == 0 else LATER_PLANE_LOADS):
+            for lo, hi in spans(PLANE_LOADS[j]):
                 nc.sync.dma_start(out=planes[j][:, lo:hi], in_=x_rows[:, j, lo:hi])
             if j == 0:
                 nc.sync.dma_start(offs_sb[:], offs)
@@ -69,9 +72,8 @@ def tile_picked_unmerge_relu_e_kernel(tc, xT, w1, res, offs, own, out):
 
         grouped = keep.tile([P, S * PACK], BF16, name="grouped", align_bytes=64)
         places = grouped[:].rearrange("p (e j) -> p e j", j=PACK)
-        later_rounding = [(lo, hi, "gpsimd" if lo == 0 else "vector") for lo, hi in spans(LATER_PLANE_LOADS)]
         for j in range(PACK):
-            for lo, hi, engine in FIRST_PLANE_ROUNDING if j == 0 else later_rounding:
+            for lo, hi, engine in ROUNDING[j]:
                 if engine == "scalar":
                     nc.scalar.activation(rounded[j][:, lo:hi], planes[j][:, lo:hi], COPY)
                 elif engine == "gpsimd":
@@ -79,13 +81,14 @@ def tile_picked_unmerge_relu_e_kernel(tc, xT, w1, res, offs, own, out):
                 else:
                     nc.vector.tensor_copy(out=rounded[j][:, lo:hi], in_=planes[j][:, lo:hi])
             if j == PACK - 1:
-                scalar_gathers = [(VECTOR_ENTRIES, S - LAST_GATHER), (S - LAST_GATHER, S)]
+                scalar_gathers = [(VECTOR_ENTRIES[j], S - LAST_GATHER), (S - LAST_GATHER, S)]
             else:
-                scalar_gathers = [(VECTOR_ENTRIES, S)]
+                scalar_gathers = [(VECTOR_ENTRIES[j], S)]
             for lo, hi in scalar_gathers:
                 nc.scalar.activation(places[:, lo:hi, j], rounded[j][:].indirect(entries(offs_sb, lo, hi)), COPY)
             nc.vector.tensor_copy(
-                out=places[:, 0:VECTOR_ENTRIES, j], in_=planes[j][:].indirect(entries(offs_sb, 0, VECTOR_ENTRIES))
+                out=places[:, 0 : VECTOR_ENTRIES[j], j],
+                in_=planes[j][:].indirect(entries(offs_sb, 0, VECTOR_ENTRIES[j])),
             )
 
         w_grouped = reused.tile([P, N, PACK], BF16, name="w_grouped", align_bytes=64, offset=W_RAW_BYTES)

@@ -31,7 +31,7 @@ ROUNDING = [
 ]
 
 STRETCH = 128
-BANKS = [(0, 256, "scalar"), (256, 512, "scalar"), (512, 768, "vector"), (768, 896, "scalar"), (896, 1024, "scalar")]
+BANKS = [(0, 256, "scalar"), (256, 512, "scalar"), (512, 768, "scalar"), (768, 896, "scalar"), (896, 1024, "scalar")]
 OUT_PIECES = [608, 736, 384, 192, 128]
 
 

@@ -20,18 +20,17 @@ PACK = 4
 LIST_ROWS = 16
 W_RAW_BYTES = PACK * N * 4
 
-VECTOR_ENTRIES = [416,416,416,416]
+VECTOR_ENTRIES = 416
 LAST_GATHER = T // 8
-PLANE_LOADS = [[1536,512],[640,768,384,256],[640,768,384,256],[640,768,384,256]]
-ROUNDING = [
-    [(0, 1024, "vector"), (1024, 1536, "scalar"), (1536, 1888, "vector"), (1888, 2048, "scalar")],
-    [(0, 640, "gpsimd"), (640, 1408, "vector"), (1408, 1792, "vector"), (1792, 2048, "vector")],
-    [(0, 640, "gpsimd"), (640, 1408, "vector"), (1408, 1792, "vector"), (1792, 2048, "vector")],
-    [(0, 640, "gpsimd"), (640, 1408, "vector"), (1408, 1792, "vector"), (1792, 2048, "vector")],
-]
+
+FIRST_PLANE_LOADS = [1536, 512]
+FIRST_PLANE_ROUNDING = [(0, 1024, "vector"), (1024, 1536, "scalar"), (1536, 1888, "vector"), (1888, 2048, "scalar")]
+MIDDLE_PLANE_LOADS = [640, 768, 384, 256]
+LAST_PLANE_LOADS = [640, 768, 384, 128, 128]
+PLANE_LOADS = [FIRST_PLANE_LOADS, MIDDLE_PLANE_LOADS, MIDDLE_PLANE_LOADS, LAST_PLANE_LOADS]
 
 STRETCH = 128
-BANKS = [(0, 256, "scalar"), (256, 512, "scalar"), (512, 768, "scalar"), (768, 896, "scalar"), (896, 1024, "scalar")]
+BANK_ENTRIES = [256, 256, 256, 128, 128]
 OUT_PIECES = [608, 736, 384, 192, 128]
 
 
@@ -73,7 +72,11 @@ def tile_picked_unmerge_relu_e_kernel(tc, xT, w1, res, offs, own, out):
         grouped = keep.tile([P, S * PACK], BF16, name="grouped", align_bytes=64)
         places = grouped[:].rearrange("p (e j) -> p e j", j=PACK)
         for j in range(PACK):
-            for lo, hi, engine in ROUNDING[j]:
+            if j == 0:
+                rounding = FIRST_PLANE_ROUNDING
+            else:
+                rounding = [(lo, hi, "gpsimd" if lo == 0 else "vector") for lo, hi in spans(PLANE_LOADS[j])]
+            for lo, hi, engine in rounding:
                 if engine == "scalar":
                     nc.scalar.activation(rounded[j][:, lo:hi], planes[j][:, lo:hi], COPY)
                 elif engine == "gpsimd":
@@ -81,14 +84,13 @@ def tile_picked_unmerge_relu_e_kernel(tc, xT, w1, res, offs, own, out):
                 else:
                     nc.vector.tensor_copy(out=rounded[j][:, lo:hi], in_=planes[j][:, lo:hi])
             if j == PACK - 1:
-                scalar_gathers = [(VECTOR_ENTRIES[j], S - LAST_GATHER), (S - LAST_GATHER, S)]
+                scalar_gathers = [(VECTOR_ENTRIES, S - LAST_GATHER), (S - LAST_GATHER, S)]
             else:
-                scalar_gathers = [(VECTOR_ENTRIES[j], S)]
+                scalar_gathers = [(VECTOR_ENTRIES, S)]
             for lo, hi in scalar_gathers:
                 nc.scalar.activation(places[:, lo:hi, j], rounded[j][:].indirect(entries(offs_sb, lo, hi)), COPY)
             nc.vector.tensor_copy(
-                out=places[:, 0 : VECTOR_ENTRIES[j], j],
-                in_=planes[j][:].indirect(entries(offs_sb, 0, VECTOR_ENTRIES[j])),
+                out=places[:, 0:VECTOR_ENTRIES, j], in_=planes[j][:].indirect(entries(offs_sb, 0, VECTOR_ENTRIES))
             )
 
         w_grouped = reused.tile([P, N, PACK], BF16, name="w_grouped", align_bytes=64, offset=W_RAW_BYTES)
@@ -100,7 +102,7 @@ def tile_picked_unmerge_relu_e_kernel(tc, xT, w1, res, offs, own, out):
         )
 
         y = keep.tile([P, S], F32, name="y")
-        for lo, hi, engine in BANKS:
+        for lo, hi in spans(BANK_ENTRIES):
             acc = psum.tile([P, hi - lo], F32, name="acc%d" % lo)
             for first in range(lo, hi, STRETCH):
                 codes = keep.tile([P, STRETCH], U32, name="codes%d" % first, align_bytes=64)
@@ -119,10 +121,7 @@ def tile_picked_unmerge_relu_e_kernel(tc, xT, w1, res, offs, own, out):
                     start=True,
                     stop=True,
                 )
-            if engine == "scalar":
-                nc.scalar.activation(y[:, lo:hi], acc[:], RELU)
-            else:
-                nc.vector.tensor_scalar_max(y[:, lo:hi], acc[:], 0.0)
+            nc.scalar.activation(y[:, lo:hi], acc[:], RELU)
 
         for lo, hi in spans(OUT_PIECES):
             result = keep.tile([P, hi - lo], F32, name="result%d" % lo)

@@ -20,18 +20,13 @@ PACK = 4
 LIST_ROWS = 16
 W_RAW_BYTES = PACK * N * 4
 
-VECTOR_ENTRIES = 416
-LAST_GATHER = T // 8
-
-FIRST_PLANE_LOADS = [1536, 512]
-FIRST_PLANE_ROUNDING = [(0, 1024, "vector"), (1024, 1536, "scalar"), (1536, 1888, "vector"), (1888, 2048, "scalar")]
-MIDDLE_PLANE_LOADS = [640, 768, 384, 256]
-LAST_PLANE_LOADS = [640, 768, 384, 128, 128]
-PLANE_LOADS = [FIRST_PLANE_LOADS, MIDDLE_PLANE_LOADS, MIDDLE_PLANE_LOADS, LAST_PLANE_LOADS]
-
+DIRECT = 480
+POOL_PIECES = [96, 96]
+LATE_PIECES = [224, 128]
 STRETCH = 128
 BANK_ENTRIES = [256, 256, 256, 128, 128]
-OUT_PIECES = [608, 736, 384, 192, 128]
+OUT_PIECES = [(320, 192), (352, 416), (192, 352), (96, 128)]
+VECTOR_ROUNDS = 1344
 
 
 def spans(widths):
@@ -57,44 +52,52 @@ def tile_picked_unmerge_relu_e_kernel(tc, xT, w1, res, offs, own, out):
         own_sb = lists.tile([P, U // LIST_ROWS], U16, name="own_sb")
 
         planes = [keep.tile([P, T], F32, name="plane%d" % j) for j in range(PACK)]
-        rounded = [keep.tile([P, T], BF16, name="rounded%d" % j) for j in range(PACK)]
         for j in range(PACK):
-            for lo, hi in spans(PLANE_LOADS[j]):
-                nc.sync.dma_start(out=planes[j][:, lo:hi], in_=x_rows[:, j, lo:hi])
+            nc.sync.dma_start(out=planes[j][:], in_=x_rows[:, j, :])
             if j == 0:
                 nc.sync.dma_start(offs_sb[:], offs)
         w_raw = reused.tile([P, PACK, N], F32, name="w_raw", align_bytes=64, offset=0)
         nc.sync.dma_start(out=w_raw[:], in_=w1.rearrange("(p j) n -> p j n", j=PACK))
         nc.sync.dma_start(own_sb[:], own)
         res_sb = keep.tile([P, U], F32, name="res_sb")
-        nc.sync.dma_start(out=res_sb[:, 0:U], in_=res[:, 0:U])
+        nc.sync.dma_start(out=res_sb[:], in_=res)
 
         grouped = keep.tile([P, S * PACK], BF16, name="grouped", align_bytes=64)
         places = grouped[:].rearrange("p (e j) -> p e j", j=PACK)
-        for j in range(PACK):
-            if j == 0:
-                rounding = FIRST_PLANE_ROUNDING
-            else:
-                rounding = [(lo, hi, "gpsimd" if lo == 0 else "vector") for lo, hi in spans(PLANE_LOADS[j])]
-            for lo, hi, engine in rounding:
-                if engine == "scalar":
-                    nc.scalar.activation(rounded[j][:, lo:hi], planes[j][:, lo:hi], COPY)
-                elif engine == "gpsimd":
-                    nc.gpsimd.tensor_copy(out=rounded[j][:, lo:hi], in_=planes[j][:, lo:hi])
-                else:
-                    nc.vector.tensor_copy(out=rounded[j][:, lo:hi], in_=planes[j][:, lo:hi])
-            if j == PACK - 1:
-                scalar_gathers = [(VECTOR_ENTRIES, S - LAST_GATHER), (S - LAST_GATHER, S)]
-            else:
-                scalar_gathers = [(VECTOR_ENTRIES, S)]
-            for lo, hi in scalar_gathers:
-                nc.scalar.activation(places[:, lo:hi, j], rounded[j][:].indirect(entries(offs_sb, lo, hi)), COPY)
-            nc.vector.tensor_copy(
-                out=places[:, 0:VECTOR_ENTRIES, j], in_=planes[j][:].indirect(entries(offs_sb, 0, VECTOR_ENTRIES))
-            )
-
         w_grouped = reused.tile([P, N, PACK], BF16, name="w_grouped", align_bytes=64, offset=W_RAW_BYTES)
-        nc.gpsimd.tensor_copy(out=w_grouped[:], in_=w_raw[:].rearrange("p j n -> p n j"))
+        late_first = DIRECT + sum(POOL_PIECES)
+        late_entries = S - late_first
+        late = keep.tile([P, PACK - 2, late_entries], BF16, name="late")
+        rounded = keep.tile([P, T], BF16, name="rounded")
+        nc.vector.tensor_copy(out=rounded[:, 0:VECTOR_ROUNDS], in_=planes[0][:, 0:VECTOR_ROUNDS])
+        nc.scalar.activation(rounded[:, VECTOR_ROUNDS:T], planes[0][:, VECTOR_ROUNDS:T], COPY)
+        nc.vector.tensor_copy(out=places[:, 0:DIRECT, 0], in_=planes[0][:].indirect(entries(offs_sb, 0, DIRECT)))
+        nc.scalar.activation(places[:, DIRECT:S, 0], rounded[:].indirect(entries(offs_sb, DIRECT, S)), COPY)
+        (early_lo, early_hi), (last_lo, last_hi) = [(DIRECT + lo, DIRECT + hi) for lo, hi in spans(POOL_PIECES)]
+        for j in range(1, PACK):
+            window = planes[j]
+            nc.vector.tensor_copy(out=places[:, 0:DIRECT, j], in_=window[:].indirect(entries(offs_sb, 0, DIRECT)))
+            picked = keep.tile([P, early_hi - early_lo], BF16, name="picked%d" % j)
+            nc.scalar.activation(picked[:], window[:].indirect(entries(offs_sb, early_lo, early_hi)), COPY)
+            nc.gpsimd.tensor_copy(out=places[:, early_lo:early_hi, j], in_=picked[:])
+            if j == PACK - 1:
+                nc.gpsimd.tensor_copy(out=w_grouped[:], in_=w_raw[:].rearrange("p j n -> p n j"))
+            slot = (j - 1) % (PACK - 2)
+            for piece, (lo, hi) in enumerate(spans(LATE_PIECES)):
+                nc.scalar.activation(
+                    late[:, slot, lo:hi], window[:].indirect(entries(offs_sb, late_first + lo, late_first + hi)), COPY
+                )
+                if piece == 0:
+                    picked_last = keep.tile([P, last_hi - last_lo], BF16, name="picked_last%d" % j)
+                    nc.scalar.activation(picked_last[:], window[:].indirect(entries(offs_sb, last_lo, last_hi)), COPY)
+                    nc.gpsimd.tensor_copy(out=places[:, last_lo:last_hi, j], in_=picked_last[:])
+            if j == PACK - 2:
+                nc.vector.tensor_copy(
+                    out=places[:, late_first:S, 1 : PACK - 1], in_=late[:].rearrange("p j e -> p e j")
+                )
+        for lo, hi in spans(LATE_PIECES):
+            nc.scalar.copy(places[:, late_first + lo : late_first + hi, PACK - 1], late[:, 0, lo:hi])
+
         w_codes = keep.tile([P, N], U32, name="w_codes", align_bytes=64)
         w_scales = keep.tile([P, N], U8, name="w_scales", align_bytes=64)
         nc.vector.quantize_mx(
@@ -123,7 +126,15 @@ def tile_picked_unmerge_relu_e_kernel(tc, xT, w1, res, offs, own, out):
                 )
             nc.scalar.activation(y[:, lo:hi], acc[:], RELU)
 
-        for lo, hi in spans(OUT_PIECES):
-            result = keep.tile([P, hi - lo], F32, name="result%d" % lo)
-            nc.vector.tensor_tensor(result[:], y[:].indirect(entries(own_sb, lo, hi)), res_sb[:, lo:hi], ADD)
-            nc.sync.dma_start(out=out[:, lo:hi], in_=result[:])
+        first = 0
+        for fused, apart in OUT_PIECES:
+            middle, end = first + fused, first + fused + apart
+            looked_up = keep.tile([P, apart], F32, name="looked_up%d" % middle)
+            nc.scalar.activation(looked_up[:], y[:].indirect(entries(own_sb, middle, end)), COPY)
+            result = keep.tile([P, fused], F32, name="result%d" % first)
+            nc.vector.tensor_tensor(result[:], y[:].indirect(entries(own_sb, first, middle)), res_sb[:, first:middle], ADD)
+            nc.sync.dma_start(out=out[:, first:middle], in_=result[:])
+            summed = keep.tile([P, apart], F32, name="summed%d" % middle)
+            nc.vector.tensor_tensor(summed[:], looked_up[:], res_sb[:, middle:end], ADD)
+            nc.sync.dma_start(out=out[:, middle:end], in_=summed[:])
+            first = end

@@ -20,13 +20,14 @@ PACK = 4
 LIST_ROWS = 16
 W_RAW_BYTES = PACK * N * 4
 
-DIRECT = 480
-POOL_PIECES = [96, 96]
-LATE_PIECES = [224, 128]
+DIRECT = 512
+MIDDLE_PIECES = [(96, "gpsimd"), (128, "gpsimd"), (160, "gpsimd"), (128, "scalar")]
+LAST_PIECES = [(96, "gpsimd"), (288, "scalar"), (128, "scalar")]
+FIRST_PLANE_LOADS = [1536, 512]
+FIRST_PLANE_ROUNDING = [(0, 1024, "vector"), (1024, 1536, "scalar"), (1536, 1888, "vector"), (1888, 2048, "scalar")]
 STRETCH = 128
-BANK_ENTRIES = [256, 256, 256, 128, 128]
-OUT_PIECES = [(320, 192), (352, 416), (192, 352), (96, 128)]
-VECTOR_ROUNDS = 1344
+BANK_ENTRIES = [384, 256, 256, 128]
+OUT_PIECES = [(320, 192), (352, 384), (224, 352), (96, 128)]
 
 
 def spans(widths):
@@ -53,7 +54,8 @@ def tile_picked_unmerge_relu_e_kernel(tc, xT, w1, res, offs, own, out):
 
         planes = [keep.tile([P, T], F32, name="plane%d" % j) for j in range(PACK)]
         for j in range(PACK):
-            nc.sync.dma_start(out=planes[j][:], in_=x_rows[:, j, :])
+            for lo, hi in spans(FIRST_PLANE_LOADS if j == 0 else [T]):
+                nc.sync.dma_start(out=planes[j][:, lo:hi], in_=x_rows[:, j, lo:hi])
             if j == 0:
                 nc.sync.dma_start(offs_sb[:], offs)
         w_raw = reused.tile([P, PACK, N], F32, name="w_raw", align_bytes=64, offset=0)
@@ -65,38 +67,32 @@ def tile_picked_unmerge_relu_e_kernel(tc, xT, w1, res, offs, own, out):
         grouped = keep.tile([P, S * PACK], BF16, name="grouped", align_bytes=64)
         places = grouped[:].rearrange("p (e j) -> p e j", j=PACK)
         w_grouped = reused.tile([P, N, PACK], BF16, name="w_grouped", align_bytes=64, offset=W_RAW_BYTES)
-        late_first = DIRECT + sum(POOL_PIECES)
-        late_entries = S - late_first
-        late = keep.tile([P, PACK - 2, late_entries], BF16, name="late")
         rounded = keep.tile([P, T], BF16, name="rounded")
-        nc.vector.tensor_copy(out=rounded[:, 0:VECTOR_ROUNDS], in_=planes[0][:, 0:VECTOR_ROUNDS])
-        nc.scalar.activation(rounded[:, VECTOR_ROUNDS:T], planes[0][:, VECTOR_ROUNDS:T], COPY)
+        for lo, hi, engine in FIRST_PLANE_ROUNDING:
+            if engine == "scalar":
+                nc.scalar.activation(rounded[:, lo:hi], planes[0][:, lo:hi], COPY)
+            else:
+                nc.vector.tensor_copy(out=rounded[:, lo:hi], in_=planes[0][:, lo:hi])
         nc.vector.tensor_copy(out=places[:, 0:DIRECT, 0], in_=planes[0][:].indirect(entries(offs_sb, 0, DIRECT)))
         nc.scalar.activation(places[:, DIRECT:S, 0], rounded[:].indirect(entries(offs_sb, DIRECT, S)), COPY)
-        (early_lo, early_hi), (last_lo, last_hi) = [(DIRECT + lo, DIRECT + hi) for lo, hi in spans(POOL_PIECES)]
+        staged = [keep.tile([P, S], BF16, name="staged%d" % slot) for slot in range(3)]
         for j in range(1, PACK):
+            last = j == PACK - 1
             window = planes[j]
             nc.vector.tensor_copy(out=places[:, 0:DIRECT, j], in_=window[:].indirect(entries(offs_sb, 0, DIRECT)))
-            picked = keep.tile([P, early_hi - early_lo], BF16, name="picked%d" % j)
-            nc.scalar.activation(picked[:], window[:].indirect(entries(offs_sb, early_lo, early_hi)), COPY)
-            nc.gpsimd.tensor_copy(out=places[:, early_lo:early_hi, j], in_=picked[:])
-            if j == PACK - 1:
-                nc.gpsimd.tensor_copy(out=w_grouped[:], in_=w_raw[:].rearrange("p j n -> p n j"))
-            slot = (j - 1) % (PACK - 2)
-            for piece, (lo, hi) in enumerate(spans(LATE_PIECES)):
-                nc.scalar.activation(
-                    late[:, slot, lo:hi], window[:].indirect(entries(offs_sb, late_first + lo, late_first + hi)), COPY
-                )
-                if piece == 0:
-                    picked_last = keep.tile([P, last_hi - last_lo], BF16, name="picked_last%d" % j)
-                    nc.scalar.activation(picked_last[:], window[:].indirect(entries(offs_sb, last_lo, last_hi)), COPY)
-                    nc.gpsimd.tensor_copy(out=places[:, last_lo:last_hi, j], in_=picked_last[:])
-            if j == PACK - 2:
-                nc.vector.tensor_copy(
-                    out=places[:, late_first:S, 1 : PACK - 1], in_=late[:].rearrange("p j e -> p e j")
-                )
-        for lo, hi in spans(LATE_PIECES):
-            nc.scalar.copy(places[:, late_first + lo : late_first + hi, PACK - 1], late[:, 0, lo:hi])
+            by_scalar = []
+            for first, end in spans([width for width, placer in (LAST_PIECES if last else MIDDLE_PIECES)]):
+                lo, hi = DIRECT + first, DIRECT + end
+                placer = [p for w, p in (LAST_PIECES if last else MIDDLE_PIECES)][len(by_scalar)]
+                stage = staged[1] if last and placer == "scalar" and hi < S else staged[j - 1]
+                nc.scalar.activation(stage[:, lo:hi], window[:].indirect(entries(offs_sb, lo, hi)), COPY)
+                if placer == "gpsimd":
+                    nc.gpsimd.tensor_copy(out=places[:, lo:hi, j], in_=stage[:, lo:hi])
+                by_scalar.append((lo, hi, placer, stage))
+            for lo, hi, placer, stage in by_scalar:
+                if placer == "scalar":
+                    nc.scalar.copy(places[:, lo:hi, j], stage[:, lo:hi])
+        nc.gpsimd.tensor_copy(out=w_grouped[:], in_=w_raw[:].rearrange("p j n -> p n j"))
 
         w_codes = keep.tile([P, N], U32, name="w_codes", align_bytes=64)
         w_scales = keep.tile([P, N], U8, name="w_scales", align_bytes=64)
@@ -105,8 +101,8 @@ def tile_picked_unmerge_relu_e_kernel(tc, xT, w1, res, offs, own, out):
         )
 
         y = keep.tile([P, S], F32, name="y")
-        for lo, hi in spans(BANK_ENTRIES):
-            acc = psum.tile([P, hi - lo], F32, name="acc%d" % lo)
+        banks = [psum.tile([P, hi - lo], F32, name="acc%d" % lo) for lo, hi in spans(BANK_ENTRIES)]
+        for acc, (lo, hi) in zip(banks, spans(BANK_ENTRIES)):
             for first in range(lo, hi, STRETCH):
                 codes = keep.tile([P, STRETCH], U32, name="codes%d" % first, align_bytes=64)
                 scales = reused.tile([P, STRETCH], U8, name="scales%d" % first, align_bytes=64, offset=first)
@@ -124,17 +120,22 @@ def tile_picked_unmerge_relu_e_kernel(tc, xT, w1, res, offs, own, out):
                     start=True,
                     stop=True,
                 )
-            nc.scalar.activation(y[:, lo:hi], acc[:], RELU)
+            if lo > 0:
+                nc.scalar.activation(y[:, lo:hi], acc[:], RELU)
+        nc.vector.tensor_relu(y[:, 0 : BANK_ENTRIES[0]], banks[0][:])
 
         first = 0
         for fused, apart in OUT_PIECES:
             middle, end = first + fused, first + fused + apart
             looked_up = keep.tile([P, apart], F32, name="looked_up%d" % middle)
             nc.scalar.activation(looked_up[:], y[:].indirect(entries(own_sb, middle, end)), COPY)
-            result = keep.tile([P, fused], F32, name="result%d" % first)
-            nc.vector.tensor_tensor(result[:], y[:].indirect(entries(own_sb, first, middle)), res_sb[:, first:middle], ADD)
-            nc.sync.dma_start(out=out[:, first:middle], in_=result[:])
-            summed = keep.tile([P, apart], F32, name="summed%d" % middle)
-            nc.vector.tensor_tensor(summed[:], looked_up[:], res_sb[:, middle:end], ADD)
-            nc.sync.dma_start(out=out[:, middle:end], in_=summed[:])
+            result = keep.tile([P, end - first], F32, name="result%d" % first)
+            nc.vector.tensor_tensor(
+                result[:, 0:fused], y[:].indirect(entries(own_sb, first, middle)), res_sb[:, first:middle], ADD
+            )
+            if first > 0:
+                nc.sync.dma_start(out=out[:, first:middle], in_=result[:, 0:fused])
+            nc.vector.tensor_tensor(result[:, fused:], looked_up[:], res_sb[:, middle:end], ADD)
+            stored = 0 if first == 0 else fused
+            nc.sync.dma_start(out=out[:, first + stored : end], in_=result[:, stored:])
             first = end

@@ -26,8 +26,19 @@ LAST_PIECES = [(96, "gpsimd"), (288, "scalar"), (128, "scalar")]
 FIRST_PLANE_LOADS = [1536, 512]
 FIRST_PLANE_ROUNDING = [(0, 1024, "vector"), (1024, 1536, "scalar"), (1536, 1888, "vector"), (1888, 2048, "scalar")]
 STRETCH = 128
-BANK_ENTRIES = [384, 256, 256, 128]
-OUT_PIECES = [(320, 192), (352, 384), (224, 352), (96, 128)]
+BANK_ENTRIES = [256, 384, 128, 128, 128]
+VECTOR_BANK = 1
+OUT_PIECES = [
+    (320, "vector"),
+    (192, "scalar"),
+    (352, "vector"),
+    (384, "scalar"),
+    (192, "vector"),
+    (288, "scalar"),
+    (192, "scalar"),
+    (128, "vector"),
+]
+NO_STORE_AFTER = [0]
 
 
 def spans(widths):
@@ -102,7 +113,8 @@ def tile_picked_unmerge_relu_e_kernel(tc, xT, w1, res, offs, own, out):
 
         y = keep.tile([P, S], F32, name="y")
         banks = [psum.tile([P, hi - lo], F32, name="acc%d" % lo) for lo, hi in spans(BANK_ENTRIES)]
-        for acc, (lo, hi) in zip(banks, spans(BANK_ENTRIES)):
+        for bank, (lo, hi) in enumerate(spans(BANK_ENTRIES)):
+            acc = banks[bank]
             for first in range(lo, hi, STRETCH):
                 codes = keep.tile([P, STRETCH], U32, name="codes%d" % first, align_bytes=64)
                 scales = reused.tile([P, STRETCH], U8, name="scales%d" % first, align_bytes=64, offset=first)
@@ -120,22 +132,21 @@ def tile_picked_unmerge_relu_e_kernel(tc, xT, w1, res, offs, own, out):
                     start=True,
                     stop=True,
                 )
-            if lo > 0:
+            if bank != VECTOR_BANK:
                 nc.scalar.activation(y[:, lo:hi], acc[:], RELU)
-        nc.vector.tensor_relu(y[:, 0 : BANK_ENTRIES[0]], banks[0][:])
+        lo, hi = spans(BANK_ENTRIES)[VECTOR_BANK]
+        nc.vector.tensor_relu(y[:, lo:hi], banks[VECTOR_BANK][:])
 
-        first = 0
-        for fused, apart in OUT_PIECES:
-            middle, end = first + fused, first + fused + apart
-            looked_up = keep.tile([P, apart], F32, name="looked_up%d" % middle)
-            nc.scalar.activation(looked_up[:], y[:].indirect(entries(own_sb, middle, end)), COPY)
-            result = keep.tile([P, end - first], F32, name="result%d" % first)
-            nc.vector.tensor_tensor(
-                result[:, 0:fused], y[:].indirect(entries(own_sb, first, middle)), res_sb[:, first:middle], ADD
-            )
-            if first > 0:
-                nc.sync.dma_start(out=out[:, first:middle], in_=result[:, 0:fused])
-            nc.vector.tensor_tensor(result[:, fused:], looked_up[:], res_sb[:, middle:end], ADD)
-            stored = 0 if first == 0 else fused
-            nc.sync.dma_start(out=out[:, first + stored : end], in_=result[:, stored:])
-            first = end
+        result = keep.tile([P, U], F32, name="result")
+        stored = 0
+        for piece, (lo, hi) in enumerate(spans([width for width, engine in OUT_PIECES])):
+            if OUT_PIECES[piece][1] == "vector":
+                looked_up = y[:].indirect(entries(own_sb, lo, hi))
+            else:
+                staged_y = keep.tile([P, hi - lo], F32, name="staged_y%d" % lo)
+                nc.scalar.activation(staged_y[:], y[:].indirect(entries(own_sb, lo, hi)), COPY)
+                looked_up = staged_y[:]
+            nc.vector.tensor_tensor(result[:, lo:hi], looked_up, res_sb[:, lo:hi], ADD)
+            if piece not in NO_STORE_AFTER:
+                nc.sync.dma_start(out=out[:, stored:hi], in_=result[:, stored:hi])
+                stored = hi

@@ -21,12 +21,12 @@ LIST_ROWS = 16
 W_RAW_BYTES = PACK * N * 4
 
 DIRECT = 512
-MIDDLE_PIECES = [(96, "gpsimd"), (128, "gpsimd"), (160, "gpsimd"), (128, "scalar")]
-LAST_PIECES = [(96, "gpsimd"), (288, "scalar"), (128, "scalar")]
+MIDDLE_PIECES = [(64, "gpsimd"), (160, "gpsimd"), (160, "gpsimd"), (128, "scalar")]
+LAST_PIECES = [(64, "gpsimd"), (320, "scalar"), (128, "scalar")]
 FIRST_PLANE_LOADS = [1536, 512]
 FIRST_PLANE_ROUNDING = [(0, 1024, "vector"), (1024, 1536, "scalar"), (1536, 1888, "vector"), (1888, 2048, "scalar")]
 STRETCH = 128
-BANK_ENTRIES = [256, 384, 128, 128, 128]
+BANK_ENTRIES = [256, 384, 128, 128, 64, 64]
 VECTOR_BANK = 1
 OUT_PIECES = [
     (320, "vector"),
@@ -90,7 +90,8 @@ def tile_picked_unmerge_relu_e_kernel(tc, xT, w1, res, offs, own, out):
         for j in range(1, PACK):
             last = j == PACK - 1
             window = planes[j]
-            nc.vector.tensor_copy(out=places[:, 0:DIRECT, j], in_=window[:].indirect(entries(offs_sb, 0, DIRECT)))
+            for lo, hi in spans([DIRECT // 2, DIRECT // 2] if last else [DIRECT]):
+                nc.vector.tensor_copy(out=places[:, lo:hi, j], in_=window[:].indirect(entries(offs_sb, lo, hi)))
             by_scalar = []
             for first, end in spans([width for width, placer in (LAST_PIECES if last else MIDDLE_PIECES)]):
                 lo, hi = DIRECT + first, DIRECT + end
@@ -116,15 +117,16 @@ def tile_picked_unmerge_relu_e_kernel(tc, xT, w1, res, offs, own, out):
         for bank, (lo, hi) in enumerate(spans(BANK_ENTRIES)):
             acc = banks[bank]
             for first in range(lo, hi, STRETCH):
-                codes = keep.tile([P, STRETCH], U32, name="codes%d" % first, align_bytes=64)
-                scales = reused.tile([P, STRETCH], U8, name="scales%d" % first, align_bytes=64, offset=first)
+                width = min(STRETCH, hi - first)
+                codes = keep.tile([P, width], U32, name="codes%d" % first, align_bytes=64)
+                scales = reused.tile([P, width], U8, name="scales%d" % first, align_bytes=64, offset=first)
                 nc.vector.quantize_mx(
                     out=codes[:].bitcast(FP8X4),
                     scales=scales[:],
-                    in_=grouped[:, PACK * first : PACK * (first + STRETCH)],
+                    in_=grouped[:, PACK * first : PACK * (first + width)],
                 )
                 nc.tensor.matmul_mx(
-                    out=acc[:, first - lo : first - lo + STRETCH],
+                    out=acc[:, first - lo : first - lo + width],
                     lhsT=w_codes[:].bitcast(FP8X4),
                     lhsT_scale=w_scales[:],
                     rhs=codes[:].bitcast(FP8X4),

@@ -20,9 +20,9 @@ PACK = 4
 LIST_ROWS = 16
 W_RAW_BYTES = PACK * N * 4
 
-DIRECT = 512
-MIDDLE_PIECES = [(64, "gpsimd"), (160, "gpsimd"), (160, "gpsimd"), (128, "scalar")]
-LAST_PIECES = [(64, "gpsimd"), (320, "scalar"), (128, "scalar")]
+DIRECT = 544
+MIDDLE_PIECES = [(64, "gpsimd"), (160, "gpsimd"), (160, "gpsimd"), (96, "scalar")]
+LAST_PIECES = [(64, "gpsimd"), (288, "scalar"), (128, "scalar")]
 FIRST_PLANE_LOADS = [1536, 512]
 FIRST_PLANE_ROUNDING = [(0, 1024, "vector"), (1024, 1536, "scalar"), (1536, 1888, "vector"), (1888, 2048, "scalar")]
 STRETCH = 128
@@ -90,7 +90,7 @@ def tile_picked_unmerge_relu_e_kernel(tc, xT, w1, res, offs, own, out):
         for j in range(1, PACK):
             last = j == PACK - 1
             window = planes[j]
-            for lo, hi in spans([DIRECT // 2, DIRECT // 2] if last else [DIRECT]):
+            for lo, hi in spans([288, 256] if last else [DIRECT]):
                 nc.vector.tensor_copy(out=places[:, lo:hi, j], in_=window[:].indirect(entries(offs_sb, lo, hi)))
             by_scalar = []
             for first, end in spans([width for width, placer in (LAST_PIECES if last else MIDDLE_PIECES)]):

@@ -21,10 +21,9 @@ LIST_ROWS = 16
 W_RAW_BYTES = PACK * N * 4
 
 DIRECT = 544
-MIDDLE_PIECES = [(64, "gpsimd"), (160, "gpsimd"), (160, "gpsimd"), (96, "scalar")]
-LAST_PIECES = [(64, "gpsimd"), (288, "scalar"), (128, "scalar")]
-FIRST_PLANE_LOADS = [1536, 512]
-FIRST_PLANE_ROUNDING = [(0, 1024, "vector"), (1024, 1536, "scalar"), (1536, 1888, "vector"), (1888, 2048, "scalar")]
+STAGED = S - DIRECT
+FIRST_PAIR_PIECES = [(96, "gpsimd"), (192, "gpsimd"), (192, "gpsimd")]
+LAST_PAIR_PIECES = [(64, "gpsimd"), (288, "scalar"), (128, "scalar")]
 STRETCH = 128
 BANK_ENTRIES = [256, 384, 128, 128, 64, 64]
 VECTOR_BANK = 1
@@ -65,8 +64,7 @@ def tile_picked_unmerge_relu_e_kernel(tc, xT, w1, res, offs, own, out):
 
         planes = [keep.tile([P, T], F32, name="plane%d" % j) for j in range(PACK)]
         for j in range(PACK):
-            for lo, hi in spans(FIRST_PLANE_LOADS if j == 0 else [T]):
-                nc.sync.dma_start(out=planes[j][:, lo:hi], in_=x_rows[:, j, lo:hi])
+            nc.sync.dma_start(out=planes[j][:], in_=x_rows[:, j, :])
             if j == 0:
                 nc.sync.dma_start(offs_sb[:], offs)
         w_raw = reused.tile([P, PACK, N], F32, name="w_raw", align_bytes=64, offset=0)
@@ -78,32 +76,26 @@ def tile_picked_unmerge_relu_e_kernel(tc, xT, w1, res, offs, own, out):
         grouped = keep.tile([P, S * PACK], BF16, name="grouped", align_bytes=64)
         places = grouped[:].rearrange("p (e j) -> p e j", j=PACK)
         w_grouped = reused.tile([P, N, PACK], BF16, name="w_grouped", align_bytes=64, offset=W_RAW_BYTES)
-        rounded = keep.tile([P, T], BF16, name="rounded")
-        for lo, hi, engine in FIRST_PLANE_ROUNDING:
-            if engine == "scalar":
-                nc.scalar.activation(rounded[:, lo:hi], planes[0][:, lo:hi], COPY)
-            else:
-                nc.vector.tensor_copy(out=rounded[:, lo:hi], in_=planes[0][:, lo:hi])
-        nc.vector.tensor_copy(out=places[:, 0:DIRECT, 0], in_=planes[0][:].indirect(entries(offs_sb, 0, DIRECT)))
-        nc.scalar.activation(places[:, DIRECT:S, 0], rounded[:].indirect(entries(offs_sb, DIRECT, S)), COPY)
-        staged = [keep.tile([P, S], BF16, name="staged%d" % slot) for slot in range(3)]
-        for j in range(1, PACK):
-            last = j == PACK - 1
-            window = planes[j]
-            for lo, hi in spans([288, 256] if last else [DIRECT]):
-                nc.vector.tensor_copy(out=places[:, lo:hi, j], in_=window[:].indirect(entries(offs_sb, lo, hi)))
-            by_scalar = []
-            for first, end in spans([width for width, placer in (LAST_PIECES if last else MIDDLE_PIECES)]):
-                lo, hi = DIRECT + first, DIRECT + end
-                placer = [p for w, p in (LAST_PIECES if last else MIDDLE_PIECES)][len(by_scalar)]
-                stage = staged[1] if last and placer == "scalar" and hi < S else staged[j - 1]
-                nc.scalar.activation(stage[:, lo:hi], window[:].indirect(entries(offs_sb, lo, hi)), COPY)
+        for pair, pieces in enumerate([FIRST_PAIR_PIECES, LAST_PAIR_PIECES]):
+            staged = keep.tile([P, 2 * STAGED], BF16, name="staged%d" % pair)
+            by_entry = staged[:].rearrange("p (h e) -> p e h", h=2)
+            for half in range(2):
+                j = 2 * pair + half
+                for lo, hi in spans([288, 256] if j == PACK - 1 else [DIRECT]):
+                    nc.vector.tensor_copy(out=places[:, lo:hi, j], in_=planes[j][:].indirect(entries(offs_sb, lo, hi)))
+                cuts = spans([width for width, placer in pieces] if half == 1 else [STAGED])
+                for lo, hi in cuts:
+                    nc.scalar.activation(
+                        staged[:, half * STAGED + lo : half * STAGED + hi],
+                        planes[j][:].indirect(entries(offs_sb, DIRECT + lo, DIRECT + hi)),
+                        COPY,
+                    )
+            for (lo, hi), (width, placer) in zip(cuts, pieces):
+                target = places[:, DIRECT + lo : DIRECT + hi, 2 * pair : 2 * pair + 2]
                 if placer == "gpsimd":
-                    nc.gpsimd.tensor_copy(out=places[:, lo:hi, j], in_=stage[:, lo:hi])
-                by_scalar.append((lo, hi, placer, stage))
-            for lo, hi, placer, stage in by_scalar:
-                if placer == "scalar":
-                    nc.scalar.copy(places[:, lo:hi, j], stage[:, lo:hi])
+                    nc.gpsimd.tensor_copy(out=target, in_=by_entry[:, lo:hi, :])
+                else:
+                    nc.scalar.copy(target, by_entry[:, lo:hi, :])
         nc.gpsimd.tensor_copy(out=w_grouped[:], in_=w_raw[:].rearrange("p j n -> p n j"))
 
         w_codes = keep.tile([P, N], U32, name="w_codes", align_bytes=64)

@@ -73,6 +73,10 @@ def tile_picked_unmerge_relu_e_kernel(tc, xT, w1, res, offs, own, out):
         res_sb = keep.tile([P, U], F32, name="res_sb")
         nc.sync.dma_start(out=res_sb[:], in_=res)
 
+        idle = keep.tile([P, 2], F32, name="idle")
+        nc.vector.memset(idle[:, 0:1], 0.0)
+        nc.scalar.activation(idle[:, 1:2], idle[:, 0:1], COPY)
+
         grouped = keep.tile([P, S * PACK], BF16, name="grouped", align_bytes=64)
         places = grouped[:].rearrange("p (e j) -> p e j", j=PACK)
         w_grouped = reused.tile([P, N, PACK], BF16, name="w_grouped", align_bytes=64, offset=W_RAW_BYTES)

@@ -19,13 +19,13 @@ P = 128
 PACK = 4
 LIST_ROWS = 16
 W_RAW_BYTES = PACK * N * 4
+RES_OFFSET = 2 * W_RAW_BYTES
 
-DIRECT = 544
-STAGED = S - DIRECT
-FIRST_PAIR_PIECES = [(96, "gpsimd"), (192, "gpsimd"), (192, "gpsimd")]
-LAST_PAIR_PIECES = [(64, "gpsimd"), (288, "scalar"), (128, "scalar")]
-STRETCH = 128
-BANK_ENTRIES = [256, 384, 128, 128, 64, 64]
+DIRECT = 608
+LATE = 64
+OWN = 960
+GPSIMD_PIECES = [(608, 768), (768, 960)]
+BANKS = [[(64, 128)], [(128, 256), (256, 384), (384, 512), (512, 640)], [(640, 768)], [(768, 896)], [(896, 1024)], [(0, 64)]]
 VECTOR_BANK = 1
 OUT_PIECES = [
     (320, "vector"),
@@ -62,7 +62,12 @@ def tile_picked_unmerge_relu_e_kernel(tc, xT, w1, res, offs, own, out):
         offs_sb = lists.tile([P, S // LIST_ROWS], U16, name="offs_sb")
         own_sb = lists.tile([P, U // LIST_ROWS], U16, name="own_sb")
 
-        planes = [keep.tile([P, T], F32, name="plane%d" % j) for j in range(PACK)]
+        planes = [
+            reused.tile([P, T], F32, name="plane%d" % j, offset=RES_OFFSET)
+            if j == PACK - 2
+            else keep.tile([P, T], F32, name="plane%d" % j)
+            for j in range(PACK)
+        ]
         for j in range(PACK):
             nc.sync.dma_start(out=planes[j][:], in_=x_rows[:, j, :])
             if j == 0:
@@ -70,36 +75,45 @@ def tile_picked_unmerge_relu_e_kernel(tc, xT, w1, res, offs, own, out):
         w_raw = reused.tile([P, PACK, N], F32, name="w_raw", align_bytes=64, offset=0)
         nc.sync.dma_start(out=w_raw[:], in_=w1.rearrange("(p j) n -> p j n", j=PACK))
         nc.sync.dma_start(own_sb[:], own)
-        res_sb = keep.tile([P, U], F32, name="res_sb")
+        res_sb = reused.tile([P, U], F32, name="res_sb", offset=RES_OFFSET)
         nc.sync.dma_start(out=res_sb[:], in_=res)
-
-        idle = keep.tile([P, 2], F32, name="idle")
-        nc.vector.memset(idle[:, 0:1], 0.0)
-        nc.scalar.activation(idle[:, 1:2], idle[:, 0:1], COPY)
 
         grouped = keep.tile([P, S * PACK], BF16, name="grouped", align_bytes=64)
         places = grouped[:].rearrange("p (e j) -> p e j", j=PACK)
         w_grouped = reused.tile([P, N, PACK], BF16, name="w_grouped", align_bytes=64, offset=W_RAW_BYTES)
-        for pair, pieces in enumerate([FIRST_PAIR_PIECES, LAST_PAIR_PIECES]):
-            staged = keep.tile([P, 2 * STAGED], BF16, name="staged%d" % pair)
-            by_entry = staged[:].rearrange("p (h e) -> p e h", h=2)
-            for half in range(2):
-                j = 2 * pair + half
-                for lo, hi in spans([288, 256] if j == PACK - 1 else [DIRECT]):
-                    nc.vector.tensor_copy(out=places[:, lo:hi, j], in_=planes[j][:].indirect(entries(offs_sb, lo, hi)))
-                cuts = spans([width for width, placer in pieces] if half == 1 else [STAGED])
-                for lo, hi in cuts:
-                    nc.scalar.activation(
-                        staged[:, half * STAGED + lo : half * STAGED + hi],
-                        planes[j][:].indirect(entries(offs_sb, DIRECT + lo, DIRECT + hi)),
-                        COPY,
-                    )
-            for (lo, hi), (width, placer) in zip(cuts, pieces):
-                target = places[:, DIRECT + lo : DIRECT + hi, 2 * pair : 2 * pair + 2]
-                if placer == "gpsimd":
-                    nc.gpsimd.tensor_copy(out=target, in_=by_entry[:, lo:hi, :])
-                else:
-                    nc.scalar.copy(target, by_entry[:, lo:hi, :])
+        def gather(target, j, lo, hi):
+            nc.scalar.activation(target, planes[j][:].indirect(entries(offs_sb, lo, hi)), COPY)
+
+        first_pair = keep.tile([P, 2 * S], BF16, name="first_pair")
+        by_entry = first_pair[:].rearrange("p (h e) -> p e h", h=2)
+        for j in range(2):
+            nc.vector.tensor_copy(out=places[:, 0:DIRECT, j], in_=planes[j][:].indirect(entries(offs_sb, 0, DIRECT)))
+            for lo, hi in [(DIRECT, S)] if j == 0 else GPSIMD_PIECES + [(OWN, S)]:
+                gather(first_pair[:, j * S + lo : j * S + hi], j, lo, hi)
+        for lo, hi in GPSIMD_PIECES:
+            nc.gpsimd.tensor_copy(out=places[:, lo:hi, 0:2], in_=by_entry[:, lo:hi, :])
+        nc.scalar.copy(places[:, OWN:S, 0:2], by_entry[:, OWN:S, :])
+
+        staged = [keep.tile([P, S], BF16, name="staged%d" % slot) for slot in range(2)]
+        late_pair = keep.tile([P, 2 * LATE], BF16, name="late_pair")
+        nc.vector.tensor_copy(out=places[:, LATE:DIRECT, 2], in_=planes[2][:].indirect(entries(offs_sb, LATE, DIRECT)))
+        for lo, hi in GPSIMD_PIECES:
+            gather(staged[0][:, lo:hi], 2, lo, hi)
+            nc.gpsimd.tensor_copy(out=places[:, lo:hi, 2], in_=staged[0][:, lo:hi])
+        gather(staged[0][:, OWN:S], 2, OWN, S)
+        gather(late_pair[:, 0:LATE], 2, 0, LATE)
+        nc.scalar.copy(places[:, OWN:S, 2], staged[0][:, OWN:S])
+
+        for lo, hi in [(LATE, 352), (352, DIRECT)]:
+            nc.vector.tensor_copy(out=places[:, lo:hi, 3], in_=planes[3][:].indirect(entries(offs_sb, lo, hi)))
+        gather(staged[1][:, DIRECT:672], 3, DIRECT, 672)
+        nc.gpsimd.tensor_copy(out=places[:, DIRECT:672, 3], in_=staged[1][:, DIRECT:672])
+        gather(staged[0][:, 672:896], 3, 672, 896)
+        gather(staged[1][:, 896:S], 3, 896, S)
+        gather(late_pair[:, LATE : 2 * LATE], 3, 0, LATE)
+        nc.scalar.copy(places[:, 672:896, 3], staged[0][:, 672:896])
+        nc.scalar.copy(places[:, 896:S, 3], staged[1][:, 896:S])
+        nc.scalar.copy(places[:, 0:LATE, 2:4], late_pair[:].rearrange("p (h e) -> p e h", h=2))
         nc.gpsimd.tensor_copy(out=w_grouped[:], in_=w_raw[:].rearrange("p j n -> p n j"))
 
         w_codes = keep.tile([P, N], U32, name="w_codes", align_bytes=64)
@@ -109,20 +123,21 @@ def tile_picked_unmerge_relu_e_kernel(tc, xT, w1, res, offs, own, out):
         )
 
         y = keep.tile([P, S], F32, name="y")
-        banks = [psum.tile([P, hi - lo], F32, name="acc%d" % lo) for lo, hi in spans(BANK_ENTRIES)]
-        for bank, (lo, hi) in enumerate(spans(BANK_ENTRIES)):
+        banks = [psum.tile([P, passes[-1][1] - passes[0][0]], F32, name="acc%d" % passes[0][0]) for passes in BANKS]
+        for bank, passes in enumerate(BANKS):
             acc = banks[bank]
-            for first in range(lo, hi, STRETCH):
-                width = min(STRETCH, hi - first)
+            lo, hi = passes[0][0], passes[-1][1]
+            for first, end in passes:
+                width = end - first
                 codes = keep.tile([P, width], U32, name="codes%d" % first, align_bytes=64)
                 scales = reused.tile([P, width], U8, name="scales%d" % first, align_bytes=64, offset=first)
                 nc.vector.quantize_mx(
                     out=codes[:].bitcast(FP8X4),
                     scales=scales[:],
-                    in_=grouped[:, PACK * first : PACK * (first + width)],
+                    in_=grouped[:, PACK * first : PACK * end],
                 )
                 nc.tensor.matmul_mx(
-                    out=acc[:, first - lo : first - lo + width],
+                    out=acc[:, first - lo : end - lo],
                     lhsT=w_codes[:].bitcast(FP8X4),
                     lhsT_scale=w_scales[:],
                     rhs=codes[:].bitcast(FP8X4),
@@ -132,7 +147,7 @@ def tile_picked_unmerge_relu_e_kernel(tc, xT, w1, res, offs, own, out):
                 )
             if bank != VECTOR_BANK:
                 nc.scalar.activation(y[:, lo:hi], acc[:], RELU)
-        lo, hi = spans(BANK_ENTRIES)[VECTOR_BANK]
+        lo, hi = BANKS[VECTOR_BANK][0][0], BANKS[VECTOR_BANK][-1][1]
         nc.vector.tensor_relu(y[:, lo:hi], banks[VECTOR_BANK][:])
 
         result = keep.tile([P, U], F32, name="result")

@@ -37,7 +37,6 @@ OUT_PIECES = [
     (192, "scalar"),
     (128, "vector"),
 ]
-NO_STORE_AFTER = [0]
 
 
 def spans(widths):
@@ -151,7 +150,6 @@ def tile_picked_unmerge_relu_e_kernel(tc, xT, w1, res, offs, own, out):
         nc.vector.tensor_relu(y[:, lo:hi], banks[VECTOR_BANK][:])
 
         result = keep.tile([P, U], F32, name="result")
-        stored = 0
         for piece, (lo, hi) in enumerate(spans([width for width, engine in OUT_PIECES])):
             if OUT_PIECES[piece][1] == "vector":
                 looked_up = y[:].indirect(entries(own_sb, lo, hi))
@@ -160,6 +158,4 @@ def tile_picked_unmerge_relu_e_kernel(tc, xT, w1, res, offs, own, out):
                 nc.scalar.activation(staged_y[:], y[:].indirect(entries(own_sb, lo, hi)), COPY)
                 looked_up = staged_y[:]
             nc.vector.tensor_tensor(result[:, lo:hi], looked_up, res_sb[:, lo:hi], ADD)
-            if piece not in NO_STORE_AFTER:
-                nc.sync.dma_start(out=out[:, stored:hi], in_=result[:, stored:hi])
-                stored = hi
+            nc.sync.dma_start(out=out[:, lo:hi], in_=result[:, lo:hi])

@@ -25,7 +25,7 @@ DIRECT = 608
 LATE = 64
 OWN = 960
 GPSIMD_PIECES = [(608, 768), (768, 960)]
-BANKS = [[(64, 128)], [(128, 256), (256, 384), (384, 512), (512, 640)], [(640, 768)], [(768, 896)], [(896, 1024)], [(0, 64)]]
+BANKS = [[(64, 128), (128, 256), (256, 384)], [(384, 512), (512, 640)], [(640, 768)], [(768, 896)], [(896, 1024)], [(0, 64)]]
 VECTOR_BANK = 1
 OUT_PIECES = [
     (320, "vector"),

@@ -32,11 +32,13 @@ OUT_PIECES = [
     (192, "scalar"),
     (352, "vector"),
     (384, "scalar"),
-    (192, "vector"),
+    (96, "vector"),
     (288, "scalar"),
+    (96, "vector"),
     (192, "scalar"),
     (128, "vector"),
 ]
+STORES = [160, 160, 192, 352, 384, 384, 288, 128]
 
 
 def spans(widths):
@@ -158,4 +160,6 @@ def tile_picked_unmerge_relu_e_kernel(tc, xT, w1, res, offs, own, out):
                 nc.scalar.activation(staged_y[:], y[:].indirect(entries(own_sb, lo, hi)), COPY)
                 looked_up = staged_y[:]
             nc.vector.tensor_tensor(result[:, lo:hi], looked_up, res_sb[:, lo:hi], ADD)
-            nc.sync.dma_start(out=out[:, lo:hi], in_=result[:, lo:hi])
+            for first, end in spans(STORES):
+                if lo < end <= hi:
+                    nc.sync.dma_start(out=out[:, first:end], in_=result[:, first:end])

@@ -27,18 +27,8 @@ OWN = 960
 GPSIMD_PIECES = [(608, 768), (768, 960)]
 BANKS = [[(64, 128), (128, 256), (256, 384)], [(384, 512), (512, 640)], [(640, 768)], [(768, 896)], [(896, 1024)], [(0, 64)]]
 VECTOR_BANK = 1
-OUT_PIECES = [
-    (320, "vector"),
-    (192, "scalar"),
-    (352, "vector"),
-    (384, "scalar"),
-    (96, "vector"),
-    (288, "scalar"),
-    (96, "vector"),
-    (192, "scalar"),
-    (128, "vector"),
-]
-STORES = [160, 160, 192, 352, 384, 384, 288, 128]
+OUT_PIECES = [(384, "vector"), (192, "scalar"), (320, "vector"), (384, "scalar"), (160, "vector"), (288, "scalar"), (192, "scalar"), (128, "vector")]
+STORES = [384, 192, 320, 384, 160, 288, 192, 128]
 
 
 def spans(widths):

from contextlib import ExitStack

import concourse.mybir as mybir

K, T, S, N, U = 512, 2048, 1024, 128, 2048
FLOPS = 2 * K * N * S

F32 = mybir.dt.float32
BF16 = mybir.dt.bfloat16
U32 = mybir.dt.uint32
U16 = mybir.dt.uint16
U8 = mybir.dt.uint8
FP8X4 = mybir.dt.float8_e4m3fn_x4
COPY = mybir.ActivationFunctionType.Copy
RELU = mybir.ActivationFunctionType.Relu
ADD = mybir.AluOpType.add

P = 128
PACK = 4
LIST_ROWS = 16
W_RAW_BYTES = PACK * N * 4
RES_OFFSET = 2 * W_RAW_BYTES

DIRECT = 608
LATE = 64
OWN = 960
GPSIMD_PIECES = [(608, 768), (768, 960)]
BANKS = [[(64, 128), (128, 256), (256, 384)], [(384, 512), (512, 640)], [(640, 768)], [(768, 896)], [(896, 1024)], [(0, 64)]]
VECTOR_BANK = 1
OUT_PIECES = [(384, "vector"), (192, "scalar"), (320, "vector"), (384, "scalar"), (160, "vector"), (288, "scalar"), (192, "scalar"), (128, "vector")]
STORES = [384, 192, 320, 384, 160, 288, 192, 128]


def spans(widths):
    edges = [sum(widths[:i]) for i in range(len(widths) + 1)]
    return [(edges[i], edges[i + 1]) for i in range(len(widths))]


def entries(list_tile, lo, hi):
    return list_tile[:, lo // LIST_ROWS : hi // LIST_ROWS]


def tile_picked_unmerge_relu_e_kernel(tc, xT, w1, res, offs, own, out):
    nc = tc.nc
    x_rows = xT.rearrange("(p j) t -> p j t", j=PACK)

    with ExitStack() as ctx:
        lists = ctx.enter_context(tc.tile_pool(name="lists", bufs=1))
        keep = ctx.enter_context(tc.tile_pool(name="keep", bufs=1))
        reused = ctx.enter_context(tc.tile_pool(name="reused", bufs=1))
        psum = ctx.enter_context(tc.psum_pool(name="psum", bufs=1))

        offs_sb = lists.tile([P, S // LIST_ROWS], U16, name="offs_sb")
        own_sb = lists.tile([P, U // LIST_ROWS], U16, name="own_sb")

        planes = [
            reused.tile([P, T], F32, name="plane%d" % j, offset=RES_OFFSET)
            if j == PACK - 2
            else keep.tile([P, T], F32, name="plane%d" % j)
            for j in range(PACK)
        ]
        for j in range(PACK):
            nc.sync.dma_start(out=planes[j][:], in_=x_rows[:, j, :])
            if j == 0:
                nc.sync.dma_start(offs_sb[:], offs)
        w_raw = reused.tile([P, PACK, N], F32, name="w_raw", align_bytes=64, offset=0)
        nc.sync.dma_start(out=w_raw[:], in_=w1.rearrange("(p j) n -> p j n", j=PACK))
        nc.sync.dma_start(own_sb[:], own)
        res_sb = reused.tile([P, U], F32, name="res_sb", offset=RES_OFFSET)
        nc.sync.dma_start(out=res_sb[:], in_=res)

        grouped = keep.tile([P, S * PACK], BF16, name="grouped", align_bytes=64)
        places = grouped[:].rearrange("p (e j) -> p e j", j=PACK)
        w_grouped = reused.tile([P, N, PACK], BF16, name="w_grouped", align_bytes=64, offset=W_RAW_BYTES)
        def gather(target, j, lo, hi):
            nc.scalar.activation(target, planes[j][:].indirect(entries(offs_sb, lo, hi)), COPY)

        first_pair = keep.tile([P, 2 * S], BF16, name="first_pair")
        by_entry = first_pair[:].rearrange("p (h e) -> p e h", h=2)
        for j in range(2):
            nc.vector.tensor_copy(out=places[:, 0:DIRECT, j], in_=planes[j][:].indirect(entries(offs_sb, 0, DIRECT)))
            for lo, hi in [(DIRECT, S)] if j == 0 else GPSIMD_PIECES + [(OWN, S)]:
                gather(first_pair[:, j * S + lo : j * S + hi], j, lo, hi)
        for lo, hi in GPSIMD_PIECES:
            nc.gpsimd.tensor_copy(out=places[:, lo:hi, 0:2], in_=by_entry[:, lo:hi, :])
        nc.scalar.copy(places[:, OWN:S, 0:2], by_entry[:, OWN:S, :])

        staged = [keep.tile([P, S], BF16, name="staged%d" % slot) for slot in range(2)]
        late_pair = keep.tile([P, 2 * LATE], BF16, name="late_pair")
        nc.vector.tensor_copy(out=places[:, LATE:DIRECT, 2], in_=planes[2][:].indirect(entries(offs_sb, LATE, DIRECT)))
        for lo, hi in GPSIMD_PIECES:
            gather(staged[0][:, lo:hi], 2, lo, hi)
            nc.gpsimd.tensor_copy(out=places[:, lo:hi, 2], in_=staged[0][:, lo:hi])
        gather(staged[0][:, OWN:S], 2, OWN, S)
        gather(late_pair[:, 0:LATE], 2, 0, LATE)
        nc.scalar.copy(places[:, OWN:S, 2], staged[0][:, OWN:S])

        for lo, hi in [(LATE, 352), (352, DIRECT)]:
            nc.vector.tensor_copy(out=places[:, lo:hi, 3], in_=planes[3][:].indirect(entries(offs_sb, lo, hi)))
        gather(staged[1][:, DIRECT:672], 3, DIRECT, 672)
        nc.gpsimd.tensor_copy(out=places[:, DIRECT:672, 3], in_=staged[1][:, DIRECT:672])
        gather(staged[0][:, 672:896], 3, 672, 896)
        gather(staged[1][:, 896:S], 3, 896, S)
        gather(late_pair[:, LATE : 2 * LATE], 3, 0, LATE)
        nc.scalar.copy(places[:, 672:896, 3], staged[0][:, 672:896])
        nc.scalar.copy(places[:, 896:S, 3], staged[1][:, 896:S])
        nc.scalar.copy(places[:, 0:LATE, 2:4], late_pair[:].rearrange("p (h e) -> p e h", h=2))
        nc.gpsimd.tensor_copy(out=w_grouped[:], in_=w_raw[:].rearrange("p j n -> p n j"))

        w_codes = keep.tile([P, N], U32, name="w_codes", align_bytes=64)
        w_scales = keep.tile([P, N], U8, name="w_scales", align_bytes=64)
        nc.vector.quantize_mx(
            out=w_codes[:].bitcast(FP8X4), scales=w_scales[:], in_=w_grouped[:].rearrange("p n j -> p (n j)")
        )

        y = keep.tile([P, S], F32, name="y")
        banks = [psum.tile([P, passes[-1][1] - passes[0][0]], F32, name="acc%d" % passes[0][0]) for passes in BANKS]
        for bank, passes in enumerate(BANKS):
            acc = banks[bank]
            lo, hi = passes[0][0], passes[-1][1]
            for first, end in passes:
                width = end - first
                codes = keep.tile([P, width], U32, name="codes%d" % first, align_bytes=64)
                scales = reused.tile([P, width], U8, name="scales%d" % first, align_bytes=64, offset=first)
                nc.vector.quantize_mx(
                    out=codes[:].bitcast(FP8X4),
                    scales=scales[:],
                    in_=grouped[:, PACK * first : PACK * end],
                )
                nc.tensor.matmul_mx(
                    out=acc[:, first - lo : end - lo],
                    lhsT=w_codes[:].bitcast(FP8X4),
                    lhsT_scale=w_scales[:],
                    rhs=codes[:].bitcast(FP8X4),
                    rhs_scale=scales[:],
                    start=True,
                    stop=True,
                )
            if bank != VECTOR_BANK:
                nc.scalar.activation(y[:, lo:hi], acc[:], RELU)
        lo, hi = BANKS[VECTOR_BANK][0][0], BANKS[VECTOR_BANK][-1][1]
        nc.vector.tensor_relu(y[:, lo:hi], banks[VECTOR_BANK][:])

        result = keep.tile([P, U], F32, name="result")
        for piece, (lo, hi) in enumerate(spans([width for width, engine in OUT_PIECES])):
            if OUT_PIECES[piece][1] == "vector":
                looked_up = y[:].indirect(entries(own_sb, lo, hi))
            else:
                staged_y = keep.tile([P, hi - lo], F32, name="staged_y%d" % lo)
                nc.scalar.activation(staged_y[:], y[:].indirect(entries(own_sb, lo, hi)), COPY)
                looked_up = staged_y[:]
            nc.vector.tensor_tensor(result[:, lo:hi], looked_up, res_sb[:, lo:hi], ADD)
            for first, end in spans(STORES):
                if lo < end <= hi:
                    nc.sync.dma_start(out=out[:, first:end], in_=result[:, first:end])
